import numpy as np
import ml_dtypes


def mxq(x, axis, fmt="e4m3"):
    dtype, down = {"e4m3": (ml_dtypes.float8_e4m3fn, 7), "e5m2": (ml_dtypes.float8_e5m2, 14)}[fmt]
    v = np.moveaxis(np.asarray(x, np.float32).astype(ml_dtypes.bfloat16).astype(np.float64), axis, -1)
    blocks = v.reshape(v.shape[:-1] + (-1, 32))
    amax = np.abs(blocks).max(-1, keepdims=True)
    byte = np.maximum(np.where(amax > 0, np.frexp(amax)[1] - 1 + 127, 0) - down, 1)
    scale = np.exp2(byte - 127.0)
    codes = (blocks / scale).astype(np.float32).astype(dtype).astype(np.float64)
    return np.moveaxis((codes * scale).reshape(v.shape), -1, axis)


WIDE = False


def mx_kscale(k):
    if not WIDE:
        return np.ones(k)
    levels = np.array([10, -10, 5, -5, 0])
    if k % 512:
        return np.exp2(np.random.permutation(np.resize(levels, k // 32))).repeat(32)
    a = np.empty((k // 512, 16))
    for p in range(k // 512):
        a[p, :8] = np.random.permutation(np.resize(levels, 8))
        for g in range(8):
            far = levels[np.abs(levels - a[p, g]) >= 10]
            a[p, g + 8] = far[np.random.randint(len(far))]
    return np.exp2(a.ravel()).repeat(32)


def f64(x):
    return np.asarray(x).astype(np.float64)


def striped(idx):
    return np.tile(idx.reshape(-1, 16).T, (8, 1)).astype(np.uint16)


def unstriped(offs):
    return offs[:16].T.reshape(-1).astype(np.int64)


def striped8(idx):
    return np.concatenate([x.reshape(-1, 16).T for x in idx]).astype(np.uint16)


def runs(offs, k):
    lists = np.stack([offs[16 * r : 16 * r + 16].T.reshape(-1) for r in range(8)]).astype(np.int64)
    return lists[np.arange(k) % 512 // 64]


def pack_weight(w):
    k, n = w.shape
    w = f64(np.asarray(w, np.float32).astype(ml_dtypes.bfloat16)).reshape(k // 32, 32, n)
    amax = np.abs(w).max(1)
    byte = np.clip(np.where(amax > 0, np.frexp(amax)[1] - 1 + 127 - 7, 1), 1, 254)
    scaled = (w * np.exp2(127.0 - byte)[:, None, :]).reshape(k, n).astype(np.float32)
    words = np.ascontiguousarray(scaled.reshape(k // 512, 128, 4, n).transpose(0, 1, 3, 2)).astype(ml_dtypes.float8_e4m3fn).view(np.uint8)
    return words, np.ascontiguousarray(byte.astype(np.uint8).reshape(k // 512, 16, n))


def unpack_weight(words, scales):
    g, p, n, _ = words.shape
    vals = np.ascontiguousarray(words).view(ml_dtypes.float8_e4m3fn).astype(np.float64) * np.repeat(np.exp2(scales.astype(np.float64) - 127.0), 8, axis=1)[..., None]
    return vals.transpose(0, 1, 3, 2).reshape(g * 512, n)


def relu(v):
    return np.maximum(v, 0.0)


def sigmoid(v):
    return 1.0 / (1.0 + np.exp(-np.maximum(v, -700.0)))


K, T, S, H, W = 512, 2048, 512, 512, 256


def setup_inputs():
    n = np.random.standard_normal
    s = mx_kscale(K)[:, None]
    u = mx_kscale(H)
    packed_xT = pack_weight(n((K, T)) * s)
    perm = np.stack([np.random.permutation(S) for _ in range(8)])
    return {
        "x_words": packed_xT[0],
        "x_scales": packed_xT[1],
        "w1": (n((K, H)) / np.sqrt(K) / s).astype(np.float32),
        "gn": (np.random.uniform(0.5, 1.5, (H, 1)) * u[:, None]).astype(np.float32),
        "w2": (n((H, H)) / np.sqrt(H) / u[:, None]).astype(np.float32),
        "offs": striped(np.random.permutation(T)[:S]),
        "n1": striped8(perm[:, :W]),
        "n2": striped8(perm[:, W:]),
        "n3": striped8(np.stack([np.random.permutation(S) for _ in range(8)])),
        "n4": striped8(np.stack([np.random.permutation(S) for _ in range(8)])),
    }


def reference(x_words, x_scales, w1, gn, w2, offs, n1, n2, n3, n4):
    xq = unpack_weight(x_words, x_scales)[:, unstriped(offs)]
    y = mxq(f64(w1), 0, "e4m3").T @ xq
    pa = y[np.arange(H)[:, None], runs(n1, H)]
    pb = y[np.arange(H)[:, None], runs(n2, H)]
    ra = pa * sigmoid(pb)
    ds = y.copy()
    ds[np.arange(H)[:, None], runs(n2, H)] = ra
    z = f64(gn) * ds
    w2q = mxq(f64(w2), 0, "e4m3")
    h = w2q.T @ mxq(z, 0, "e4m3")
    z2 = f64(gn) * (relu(h - (h[np.arange(H)[:, None], runs(n3, H)])) + 0.5 * (relu(h[np.arange(H)[:, None], runs(n4, H)] - h)))
    return (w2q.T @ mxq(z2, 0, "e4m3")) + 1.5 * y

@@ -1,0 +1,230 @@
+from contextlib import ExitStack
+
+import concourse.mybir as mybir
+
+K, T, S, H, W = 512, 2048, 512, 512, 256
+FLOPS = 3 * 2 * 512 * 512 * 512
+
+F32 = mybir.dt.float32
+BF16 = mybir.dt.bfloat16
+I32 = mybir.dt.int32
+U32 = mybir.dt.uint32
+U16 = mybir.dt.uint16
+U8 = mybir.dt.uint8
+FP8X4 = mybir.dt.float8_e4m3fn_x4
+ALU = mybir.AluOpType
+ACT = mybir.ActivationFunctionType
+
+P = 128
+PACK = 4
+HALF = S // 2
+QUARTER = S // 4
+W1_VECTOR_M = 64
+W2_PIECES = 8
+
+
+def tile_picked_iterfoldhinge_none_p_kernel(
+    tc, x_words, x_scales, w1, gn, w2, offs, n1, n2, n3, n4, out
+):
+    nc = tc.nc
+    with ExitStack() as ctx:
+        keep = ctx.enter_context(tc.tile_pool(name="keep", bufs=1))
+        psum = ctx.enter_context(tc.psum_pool(name="psum", bufs=1))
+
+        def sbuf(name, shape, dtype, tag=None):
+            return keep.tile(shape, dtype, name=name, tag=tag or name, align_bytes=64)
+
+        def bank(index, shape):
+            return psum.tile(shape, F32, name="bank%d" % index)
+
+        offs_t = sbuf("offs_t", [P, S // 16], U16)
+        n1_t = sbuf("n1_t", [P, W // 16], U16)
+        n2_t = sbuf("n2_t", [P, W // 16], U16)
+        n3_t = sbuf("n3_t", [P, S // 16], U16)
+        n4_t = sbuf("n4_t", [P, S // 16], U16)
+        w1_raw = sbuf("w1_raw", [P, PACK, H], F32, tag="w_raw")
+        x_all = sbuf("x_all", [P, T], I32)
+        xs_all = sbuf("xs_all", [P, T], U8)
+        gain = sbuf("gain", [P, PACK], F32)
+        warm_in = sbuf("warm_in", [P, 1], F32)
+        warm_out = sbuf("warm_out", [P, 1], F32)
+
+        nc.vector.memset(xs_all[:].bitcast(I32), 0)
+        nc.vector.memset(warm_in[:], 0.0)
+        nc.sync.dma_start(n1_t[:], n1)
+        nc.sync.dma_start(n2_t[:], n2)
+        nc.sync.dma_start(offs_t[:], offs)
+        nc.sync.dma_start(w1_raw[:], w1.rearrange("(p j) c -> p j c", j=PACK))
+        nc.sync.dma_start(x_all[:], x_words[0].rearrange("p n t -> p (n t)").bitcast(I32))
+        nc.sync.dma_start(n3_t[:], n3)
+        nc.sync.dma_start(n4_t[:], n4)
+        for q in range(4):
+            nc.scalar.dma_start(
+                xs_all[32 * q : 32 * q + 4, :].bitcast(I32), x_scales[0, 4 * q : 4 * q + 4, :].bitcast(I32)
+            )
+        nc.scalar.activation(warm_out[:], warm_in[:], ACT.Sigmoid)
+        nc.gpsimd.dma_start(gain[:], gn.rearrange("(p t) o -> p (t o)", t=PACK))
+
+        xs = sbuf("xs", [P, S], U8)
+        nc.vector.tensor_copy(xs[:], xs_all[:].indirect(offs_t[:]))
+
+        def deal(engine_copy, grouped, rows, m0, m1):
+            engine_copy(
+                grouped[:].rearrange("p (t m j) -> p m t j", t=PACK, j=PACK)[:, m0:m1],
+                rows[:].rearrange("p j (m t) -> p m t j", t=PACK)[:, m0:m1],
+            )
+
+        w1_b = sbuf("w1_b", [P, PACK * H], BF16)
+        deal(nc.vector.tensor_copy, w1_b, w1_raw, 0, W1_VECTOR_M)
+        deal(nc.scalar.copy, w1_b, w1_raw, W1_VECTOR_M, P)
+        w1_q = sbuf("w1_q", [P, H], U32)
+        w1_s = sbuf("w1_s", [P, H], U8)
+        nc.vector.quantize_mx(out=w1_q[:].bitcast(FP8X4), scales=w1_s[:], in_=w1_b[:])
+
+        w2_raw = sbuf("w2_raw", [P, PACK, H], F32, tag="w_raw")
+        nc.sync.dma_start(w2_raw[:], w2.rearrange("(p j) c -> p j c", j=PACK))
+
+        two = sbuf("two", [P, PACK], F32)
+        sign = sbuf("sign", [P, PACK], F32)
+        size = sbuf("size", [P, PACK], F32)
+        neg_size = sbuf("neg_size", [P, PACK], F32)
+        nc.gpsimd.tensor_scalar(two[:], gain[:], 0.0, 2.0, ALU.is_ge, ALU.mult)
+        nc.gpsimd.tensor_scalar(sign[:], two[:], 1.0, -1.0, ALU.mult, ALU.add)
+        nc.gpsimd.tensor_tensor(size[:], gain[:], sign[:], ALU.mult)
+        nc.gpsimd.tensor_scalar(neg_size[:], size[:], -1.0, 0.0, ALU.mult, ALU.add)
+
+        def product(dst, wq, ws, t, rq, rs):
+            nc.tensor.matmul_mx(
+                out=dst,
+                lhsT=wq[:, t * P : (t + 1) * P].bitcast(FP8X4),
+                lhsT_scale=ws[:, t * P : (t + 1) * P],
+                rhs=rq.bitcast(FP8X4),
+                rhs_scale=rs,
+                start=True,
+                stop=True,
+            )
+
+        halves = [slice(u * HALF, (u + 1) * HALF) for u in range(2)]
+        xq = [sbuf("xq%d" % u, [P, HALF], U32) for u in range(2)]
+        y_ps = [[bank(2 * t + u, [P, HALF]) for u in range(2)] for t in range(PACK)]
+        ds = [sbuf("ds%d" % t, [P, S], F32) for t in range(PACK)]
+        for u in range(2):
+            nc.vector.tensor_copy(xq[u][:], x_all[:].bitcast(U32).indirect(offs_t[:, u * 16 : (u + 1) * 16]))
+            for t in range(PACK):
+                product(y_ps[t][u][:], w1_q, w1_s, t, xq[u][:], xs[:, halves[u]])
+
+        z_planes = sbuf("z_planes", [P, PACK, S], BF16)
+        w2_b = sbuf("w2_b", [P, PACK * H], BF16)
+        w2_q = sbuf("w2_q", [P, H], U32)
+        w2_s = sbuf("w2_s", [P, H], U8)
+        y_keep = sbuf("y_keep", [P, PACK, S], F32)
+        for t in range(PACK):
+            for u in range(2):
+                nc.scalar.copy(ds[t][:, halves[u]], y_ps[t][u][:])
+            gate = sbuf("gate%d" % t, [P, W], F32)
+            pa = sbuf("pa%d" % t, [P, W], F32)
+            nc.scalar.activation(gate[:], ds[t][:].indirect(n2_t[:]), ACT.Sigmoid)
+            if t == 0:
+                nc.vector.tensor_copy(pa[:], ds[t][:].indirect(n1_t[:]))
+                nc.vector.tensor_tensor(ds[t][:].indirect(n2_t[:]), pa[:], gate[:], ALU.mult)
+            else:
+                nc.vector.tensor_tensor(pa[:], ds[t][:].indirect(n1_t[:]), gate[:], ALU.mult)
+                nc.vector.tensor_copy(ds[t][:].indirect(n2_t[:]), pa[:])
+        for t in range(PACK):
+            for u in range(2):
+                nc.scalar.copy(y_keep[:, t, halves[u]], y_ps[t][u][:])
+        m_step = P // W2_PIECES
+        for m0 in range(0, P, m_step):
+            nc.gpsimd.tensor_tensor(
+                w2_b[:].rearrange("p (t m j) -> p m t j", t=PACK, j=PACK)[:, m0 : m0 + m_step],
+                w2_raw[:].rearrange("p j (m t) -> p m t j", t=PACK)[:, m0 : m0 + m_step],
+                sign[:].unsqueeze(1).unsqueeze(1).to_broadcast([P, m_step, PACK, PACK]),
+                ALU.mult,
+            )
+        for t in range(PACK - 1):
+            nc.scalar.activation(z_planes[:, t, :], ds[t][:], ACT.Copy, scale=size[:, t : t + 1])
+        t = PACK - 1
+        for u in range(2):
+            nc.scalar.activation(z_planes[:, t, halves[u]], ds[t][:, halves[u]], ACT.Copy, scale=size[:, t : t + 1])
+        nc.vector.quantize_mx(out=w2_q[:].bitcast(FP8X4), scales=w2_s[:], in_=w2_b[:])
+
+        z_b = [sbuf("z_b%d" % u, [P, HALF, PACK], BF16) for u in range(2)]
+        z_q = [sbuf("z_q%d" % u, [P, HALF], U32) for u in range(2)]
+        z_s = [sbuf("z_s%d" % u, [P, HALF], U8) for u in range(2)]
+        nc.vector.tensor_copy(z_b[0][:], z_planes[:, :, halves[0]].rearrange("p t c -> p c t"))
+        nc.scalar.copy(z_b[1][:], z_planes[:, :, halves[1]].rearrange("p t c -> p c t"))
+        h_ps = [[bank(2 * t + u, [P, HALF]) for u in range(2)] for t in range(PACK)]
+        for u in range(2):
+            nc.vector.quantize_mx(
+                out=z_q[u][:].bitcast(FP8X4), scales=z_s[u][:], in_=z_b[u][:].rearrange("p c t -> p (c t)")
+            )
+        for t in range(PACK):
+            for u in range(2):
+                product(h_ps[t][u][:], w2_q, w2_s, t, z_q[u][:], z_s[u][:])
+
+        window = [sbuf("window%d" % t, [P, S], F32) for t in range(PACK)]
+        plain = [[sbuf("plain%d_%d" % (t, u), [P, HALF], F32) for u in range(2)] for t in range(PACK)]
+        for t in range(PACK):
+            scale = neg_size[:, t : t + 1]
+            nc.scalar.activation(window[t][:, halves[0]], h_ps[t][0][:], ACT.Copy, scale=scale)
+            nc.scalar.activation(plain[t][0][:], h_ps[t][0][:], ACT.Copy, scale=scale)
+            nc.scalar.activation(window[t][:, halves[1]], h_ps[t][1][:], ACT.Copy, scale=scale)
+            nc.sync.dma_start(plain[t][1][:], window[t][:, halves[1]])
+
+        out_rows = out.rearrange("(p t) s -> p t s", t=PACK)
+
+        def differences(dst, list_t, t, u):
+            nc.vector.tensor_tensor(
+                dst, window[t][:].indirect(list_t[:, u * 16 : (u + 1) * 16]), plain[t][u][:], ALU.subtract
+            )
+
+        def quantise(name, planes, n, interleave, tag=None):
+            grouped = sbuf(name + "_b", [P, n, PACK], BF16, tag=tag)
+            codes = sbuf(name + "_q", [P, n], U32)
+            scales = sbuf(name + "_s", [P, n], U8)
+            interleave(grouped[:], planes.rearrange("p t c -> p c t"))
+            nc.vector.quantize_mx(
+                out=codes[:].bitcast(FP8X4), scales=scales[:], in_=grouped[:].rearrange("p c t -> p (c t)")
+            )
+            return codes, scales
+
+        def finish(name, codes, scales, bank_index, t0, t1, a, b):
+            o_ps = bank(bank_index, [P, t1 - t0, b - a])
+            res = sbuf(name, [P, t1 - t0, b - a], F32)
+            for t in range(t0, t1):
+                product(o_ps[:, t - t0, :], w2_q, w2_s, t, codes[:], scales[:])
+            nc.vector.scalar_tensor_tensor(res[:], y_keep[:, t0:t1, a:b], 1.5, o_ps[:], ALU.mult, ALU.add)
+            nc.sync.dma_start(out_rows[:, t0:t1, a:b], res[:])
+
+        e4 = sbuf("e4_first", [P, PACK, HALF], F32)
+        e3 = sbuf("e3_first", [P, PACK, HALF], F32, tag="e_shared")
+        r4 = sbuf("r4_first", [P, PACK, HALF], F32)
+        planes = sbuf("planes_first", [P, PACK, HALF], BF16)
+        for t in range(PACK):
+            differences(e4[:, t, :], n4_t, t, 0)
+        nc.scalar.activation(r4[:], e4[:], ACT.Relu, scale=-0.5)
+        for t in range(PACK):
+            differences(e3[:, t, :], n3_t, t, 0)
+        nc.vector.scalar_tensor_tensor(planes[:], e3[:], 0.0, r4[:], ALU.max, ALU.add)
+        codes, scales = quantise("z2_first", planes[:], HALF, nc.scalar.copy, tag="grouped_shared")
+        for r in range(2):
+            finish("res_first%d" % r, codes, scales, 4 * r, 2 * r, 2 * r + 2, 0, HALF)
+
+        e4 = sbuf("e4_second", [P, PACK, HALF], F32, tag="e_shared")
+        e3 = sbuf("e3_second", [P, PACK, HALF], F32, tag="grouped_shared")
+        r4 = sbuf("r4_second", [P, PACK, HALF], F32)
+        for t in range(PACK):
+            differences(e4[:, t, :], n4_t, t, 1)
+        nc.scalar.activation(r4[:], e4[:], ACT.Relu, scale=-0.5)
+        for t in range(PACK):
+            differences(e3[:, t, :], n3_t, t, 1)
+        packed = []
+        for v in range(2):
+            cols = slice(v * QUARTER, (v + 1) * QUARTER)
+            planes = sbuf("planes_second%d" % v, [P, PACK, QUARTER], BF16)
+            nc.vector.scalar_tensor_tensor(planes[:], e3[:, :, cols], 0.0, r4[:, :, cols], ALU.max, ALU.add)
+            interleave = nc.scalar.copy if v == 0 else nc.vector.tensor_copy
+            packed.append(quantise("z2_second%d" % v, planes[:], QUARTER, interleave))
+        for v in range(2):
+            a = HALF + v * QUARTER
+            finish("res_second%d" % v, packed[v][0], packed[v][1], 2 + 4 * v, 0, PACK, a, a + QUARTER)

@@ -20,7 +20,6 @@ PACK = 4
 HALF = S // 2
 QUARTER = S // 4
 W1_VECTOR_M = 64
-W2_PIECES = 8
 
 
 def tile_picked_iterfoldhinge_none_p_kernel(
@@ -49,19 +48,20 @@ def tile_picked_iterfoldhinge_none_p_kernel(
         warm_in = sbuf("warm_in", [P, 1], F32)
         warm_out = sbuf("warm_out", [P, 1], F32)
 
-        nc.vector.memset(xs_all[:].bitcast(I32), 0)
-        nc.vector.memset(warm_in[:], 0.0)
-        nc.sync.dma_start(n1_t[:], n1)
-        nc.sync.dma_start(n2_t[:], n2)
+        xs_rows = sbuf("xs_rows", [P, T // 4], I32)
+        for q in range(4):
+            nc.sync.dma_start(xs_rows[32 * q : 32 * q + 4, :], x_scales[0, 4 * q : 4 * q + 4, :].bitcast(I32))
         nc.sync.dma_start(offs_t[:], offs)
         nc.sync.dma_start(w1_raw[:], w1.rearrange("(p j) c -> p j c", j=PACK))
         nc.sync.dma_start(x_all[:], x_words[0].rearrange("p n t -> p (n t)").bitcast(I32))
+        nc.sync.dma_start(n1_t[:], n1)
+        nc.sync.dma_start(n2_t[:], n2)
         nc.sync.dma_start(n3_t[:], n3)
         nc.sync.dma_start(n4_t[:], n4)
+        nc.vector.memset(warm_in[:], 0.0)
+        nc.vector.memset(xs_all[:].bitcast(I32), 0)
         for q in range(4):
-            nc.scalar.dma_start(
-                xs_all[32 * q : 32 * q + 4, :].bitcast(I32), x_scales[0, 4 * q : 4 * q + 4, :].bitcast(I32)
-            )
+            nc.vector.tensor_copy(xs_all[32 * q : 32 * q + 4, :].bitcast(I32), xs_rows[32 * q : 32 * q + 4, :])
         nc.scalar.activation(warm_out[:], warm_in[:], ACT.Sigmoid)
         nc.gpsimd.dma_start(gain[:], gn.rearrange("(p t) o -> p (t o)", t=PACK))
 
@@ -84,6 +84,7 @@ def tile_picked_iterfoldhinge_none_p_kernel(
         w2_raw = sbuf("w2_raw", [P, PACK, H], F32, tag="w_raw")
         nc.sync.dma_start(w2_raw[:], w2.rearrange("(p j) c -> p j c", j=PACK))
 
+        w1_tiles = [(w1_q[:, t * P : (t + 1) * P], w1_s[:, t * P : (t + 1) * P]) for t in range(PACK)]
         two = sbuf("two", [P, PACK], F32)
         sign = sbuf("sign", [P, PACK], F32)
         size = sbuf("size", [P, PACK], F32)
@@ -93,11 +94,11 @@ def tile_picked_iterfoldhinge_none_p_kernel(
         nc.gpsimd.tensor_tensor(size[:], gain[:], sign[:], ALU.mult)
         nc.gpsimd.tensor_scalar(neg_size[:], size[:], -1.0, 0.0, ALU.mult, ALU.add)
 
-        def product(dst, wq, ws, t, rq, rs):
+        def product(dst, weights, rq, rs):
             nc.tensor.matmul_mx(
                 out=dst,
-                lhsT=wq[:, t * P : (t + 1) * P].bitcast(FP8X4),
-                lhsT_scale=ws[:, t * P : (t + 1) * P],
+                lhsT=weights[0].bitcast(FP8X4),
+                lhsT_scale=weights[1],
                 rhs=rq.bitcast(FP8X4),
                 rhs_scale=rs,
                 start=True,
@@ -105,126 +106,149 @@ def tile_picked_iterfoldhinge_none_p_kernel(
             )
 
         halves = [slice(u * HALF, (u + 1) * HALF) for u in range(2)]
-        xq = [sbuf("xq%d" % u, [P, HALF], U32) for u in range(2)]
-        y_ps = [[bank(2 * t + u, [P, HALF]) for u in range(2)] for t in range(PACK)]
-        ds = [sbuf("ds%d" % t, [P, S], F32) for t in range(PACK)]
+        pieces = [(0, halves[0]), (0, halves[1])] + [(t, slice(0, S)) for t in range(1, PACK)]
+        xq = sbuf("xq", [P, S], U32)
         for u in range(2):
-            nc.vector.tensor_copy(xq[u][:], x_all[:].bitcast(U32).indirect(offs_t[:, u * 16 : (u + 1) * 16]))
-            for t in range(PACK):
-                product(y_ps[t][u][:], w1_q, w1_s, t, xq[u][:], xs[:, halves[u]])
+            nc.vector.tensor_copy(xq[:, halves[u]], x_all[:].bitcast(U32).indirect(offs_t[:, u * 16 : (u + 1) * 16]))
+        y_ps = [bank(i, [P, cols.stop - cols.start]) for i, (t, cols) in enumerate(pieces)]
+        for (t, cols), ps in zip(pieces, y_ps):
+            product(ps[:], w1_tiles[t], xq[:, cols], xs[:, cols])
 
-        z_planes = sbuf("z_planes", [P, PACK, S], BF16)
+        ds = [sbuf("ds%d" % t, [P, S], F32) for t in range(PACK)]
+        w2_signed = sbuf("w2_signed", [P, PACK, H], BF16, tag="planes")
         w2_b = sbuf("w2_b", [P, PACK * H], BF16)
-        w2_q = sbuf("w2_q", [P, H], U32)
-        w2_s = sbuf("w2_s", [P, H], U8)
-        y_keep = sbuf("y_keep", [P, PACK, S], F32)
-        for t in range(PACK):
-            for u in range(2):
-                nc.scalar.copy(ds[t][:, halves[u]], y_ps[t][u][:])
-            gate = sbuf("gate%d" % t, [P, W], F32)
-            pa = sbuf("pa%d" % t, [P, W], F32)
-            nc.scalar.activation(gate[:], ds[t][:].indirect(n2_t[:]), ACT.Sigmoid)
-            if t == 0:
-                nc.vector.tensor_copy(pa[:], ds[t][:].indirect(n1_t[:]))
-                nc.vector.tensor_tensor(ds[t][:].indirect(n2_t[:]), pa[:], gate[:], ALU.mult)
-            else:
-                nc.vector.tensor_tensor(pa[:], ds[t][:].indirect(n1_t[:]), gate[:], ALU.mult)
-                nc.vector.tensor_copy(ds[t][:].indirect(n2_t[:]), pa[:])
-        for t in range(PACK):
-            for u in range(2):
-                nc.scalar.copy(y_keep[:, t, halves[u]], y_ps[t][u][:])
-        m_step = P // W2_PIECES
-        for m0 in range(0, P, m_step):
-            nc.gpsimd.tensor_tensor(
-                w2_b[:].rearrange("p (t m j) -> p m t j", t=PACK, j=PACK)[:, m0 : m0 + m_step],
-                w2_raw[:].rearrange("p j (m t) -> p m t j", t=PACK)[:, m0 : m0 + m_step],
-                sign[:].unsqueeze(1).unsqueeze(1).to_broadcast([P, m_step, PACK, PACK]),
-                ALU.mult,
-            )
+        y_first = sbuf("y_first", [P, S], F32)
+        gate = [sbuf("gate%d" % t, [P, W], F32) for t in range(PACK)]
+        pa = [sbuf("pa%d" % t, [P, W], F32) for t in range(PACK)]
+
+        def fetch(t):
+            for (tt, cols), ps in zip(pieces, y_ps):
+                if tt == t:
+                    nc.scalar.copy(ds[t][:, cols], ps[:])
+            nc.vector.tensor_copy(pa[t][:], ds[t][:].indirect(n1_t[:]))
+
+        def fold(t):
+            nc.scalar.activation(gate[t][:], ds[t][:].indirect(n2_t[:]), ACT.Sigmoid)
+            nc.vector.tensor_tensor(ds[t][:].indirect(n2_t[:]), pa[t][:], gate[t][:], ALU.mult)
+
+        fetch(0)
+        fold(0)
+        fetch(1)
+        for t in range(1, PACK):
+            if t + 1 < PACK:
+                fetch(t + 1)
+            fold(t)
+        for u in range(2):
+            nc.scalar.copy(y_first[:, halves[u]], y_ps[u][:])
+        for j in range(PACK):
+            nc.gpsimd.tensor_scalar(w2_signed[:, j, :], w2_raw[:, j, :], sign[:, j : j + 1], 0.0, ALU.mult, ALU.add)
+        deal(nc.scalar.copy, w2_b, w2_signed, 0, P)
+        z_planes = sbuf("z_planes", [P, PACK, S], BF16, tag="planes")
         for t in range(PACK - 1):
             nc.scalar.activation(z_planes[:, t, :], ds[t][:], ACT.Copy, scale=size[:, t : t + 1])
         t = PACK - 1
         for u in range(2):
             nc.scalar.activation(z_planes[:, t, halves[u]], ds[t][:, halves[u]], ACT.Copy, scale=size[:, t : t + 1])
-        nc.vector.quantize_mx(out=w2_q[:].bitcast(FP8X4), scales=w2_s[:], in_=w2_b[:])
+        w2_q0 = sbuf("w2_q0", [P, P], U32)
+        w2_s0 = sbuf("w2_s0", [P, P], U8)
+        nc.vector.quantize_mx(out=w2_q0[:].bitcast(FP8X4), scales=w2_s0[:], in_=w2_b[:, 0 : PACK * P])
 
-        z_b = [sbuf("z_b%d" % u, [P, HALF, PACK], BF16) for u in range(2)]
-        z_q = [sbuf("z_q%d" % u, [P, HALF], U32) for u in range(2)]
-        z_s = [sbuf("z_s%d" % u, [P, HALF], U8) for u in range(2)]
-        nc.vector.tensor_copy(z_b[0][:], z_planes[:, :, halves[0]].rearrange("p t c -> p c t"))
-        nc.scalar.copy(z_b[1][:], z_planes[:, :, halves[1]].rearrange("p t c -> p c t"))
-        h_ps = [[bank(2 * t + u, [P, HALF]) for u in range(2)] for t in range(PACK)]
+        z_b = [sbuf("z_b%d" % u, [P, HALF, PACK], BF16, tag="z_b%d" % u) for u in range(2)]
+        z_q = sbuf("z_q", [P, S], U32)
+        z_s = sbuf("z_s", [P, S], U8)
+        z_cols = z_planes[:].rearrange("p t c -> p c t")
+        nc.vector.tensor_copy(z_b[0][:], z_cols[:, halves[0]])
+        nc.scalar.copy(z_b[1][:, 0:QUARTER], z_cols[:, HALF : HALF + QUARTER])
+        nc.vector.tensor_copy(z_b[1][:, QUARTER:HALF], z_cols[:, HALF + QUARTER : S])
         for u in range(2):
             nc.vector.quantize_mx(
-                out=z_q[u][:].bitcast(FP8X4), scales=z_s[u][:], in_=z_b[u][:].rearrange("p c t -> p (c t)")
+                out=z_q[:, halves[u]].bitcast(FP8X4),
+                scales=z_s[:, halves[u]],
+                in_=z_b[u][:].rearrange("p c t -> p (c t)"),
             )
-        for t in range(PACK):
-            for u in range(2):
-                product(h_ps[t][u][:], w2_q, w2_s, t, z_q[u][:], z_s[u][:])
+        w2_q = sbuf("w2_q", [P, H - P], U32, tag="z_b1")
+        w2_s = sbuf("w2_s", [P, H - P], U8)
+        nc.vector.quantize_mx(out=w2_q[:, 0:P].bitcast(FP8X4), scales=w2_s[:, 0:P], in_=w2_b[:, PACK * P : 2 * PACK * P])
+        nc.vector.quantize_mx(out=w2_q[:, P:].bitcast(FP8X4), scales=w2_s[:, P:], in_=w2_b[:, 2 * PACK * P :])
+        w2_tiles = [(w2_q0[:], w2_s0[:])]
+        w2_tiles.extend((w2_q[:, t * P : (t + 1) * P], w2_s[:, t * P : (t + 1) * P]) for t in range(PACK - 1))
+        h_banks = (0, 1, 5, 6, 7)
+        h_ps = [bank(i, [P, cols.stop - cols.start]) for i, (t, cols) in zip(h_banks, pieces)]
+        for (t, cols), ps in zip(pieces, h_ps):
+            product(ps[:], w2_tiles[t], z_q[:, cols], z_s[:, cols])
 
         window = [sbuf("window%d" % t, [P, S], F32) for t in range(PACK)]
         plain = [[sbuf("plain%d_%d" % (t, u), [P, HALF], F32) for u in range(2)] for t in range(PACK)]
-        for t in range(PACK):
+        for (t, cols), ps in zip(pieces, h_ps):
             scale = neg_size[:, t : t + 1]
-            nc.scalar.activation(window[t][:, halves[0]], h_ps[t][0][:], ACT.Copy, scale=scale)
-            nc.scalar.activation(plain[t][0][:], h_ps[t][0][:], ACT.Copy, scale=scale)
-            nc.scalar.activation(window[t][:, halves[1]], h_ps[t][1][:], ACT.Copy, scale=scale)
-            nc.sync.dma_start(plain[t][1][:], window[t][:, halves[1]])
+            nc.scalar.activation(window[t][:, cols], ps[:], ACT.Copy, scale=scale)
+            if cols.start == 0 and t == 0:
+                nc.vector.tensor_copy(plain[t][0][:], window[t][:, halves[0]])
+            elif cols.start == 0:
+                nc.scalar.activation(plain[t][0][:], ps[:, halves[0]], ACT.Copy, scale=scale)
+            if cols.stop == S:
+                nc.sync.dma_start(plain[t][1][:], window[t][:, halves[1]])
 
         out_rows = out.rearrange("(p t) s -> p t s", t=PACK)
+        plane_groups = (slice(0, PACK - 1), slice(PACK - 1, PACK))
 
         def differences(dst, list_t, t, u):
             nc.vector.tensor_tensor(
                 dst, window[t][:].indirect(list_t[:, u * 16 : (u + 1) * 16]), plain[t][u][:], ALU.subtract
             )
 
-        def quantise(name, planes, n, interleave, tag=None):
-            grouped = sbuf(name + "_b", [P, n, PACK], BF16, tag=tag)
+        def hinge(name, u, e4_tag, e3_tag):
+            e4 = sbuf(name + "_e4", [P, PACK, HALF], F32, tag=e4_tag)
+            e3 = sbuf(name + "_e3", [P, PACK, HALF], F32, tag=e3_tag)
+            r4 = sbuf(name + "_r4", [P, PACK, HALF], F32)
+            planes = sbuf(name + "_planes", [P, PACK, HALF], BF16)
+            for t in range(PACK):
+                differences(e4[:, t, :], n4_t, t, u)
+            for g in plane_groups:
+                nc.scalar.activation(r4[:, g, :], e4[:, g, :], ACT.Relu, scale=-0.5)
+            for t in range(PACK):
+                differences(e3[:, t, :], n3_t, t, u)
+            for g in plane_groups:
+                nc.vector.scalar_tensor_tensor(planes[:, g, :], e3[:, g, :], 0.0, r4[:, g, :], ALU.max, ALU.add)
+            return planes
+
+        def interleave(name, planes, n, copy, tag=None):
+            grouped = sbuf(name, [P, n, PACK], BF16, tag=tag)
+            copy(grouped[:], planes.rearrange("p t c -> p c t"))
+            return grouped
+
+        def last_product(name, grouped, n, banks):
             codes = sbuf(name + "_q", [P, n], U32)
             scales = sbuf(name + "_s", [P, n], U8)
-            interleave(grouped[:], planes.rearrange("p t c -> p c t"))
             nc.vector.quantize_mx(
                 out=codes[:].bitcast(FP8X4), scales=scales[:], in_=grouped[:].rearrange("p c t -> p (c t)")
             )
-            return codes, scales
+            per_bank = PACK // len(banks)
+            sums = [bank(i, [P, per_bank, n]) for i in banks]
+            for t in range(PACK):
+                product(sums[t // per_bank][:, t % per_bank, :], w2_tiles[t], codes[:], scales[:])
+            return sums
 
-        def finish(name, codes, scales, bank_index, t0, t1, a, b):
-            o_ps = bank(bank_index, [P, t1 - t0, b - a])
+        def finish(name, sums, t0, t1, a, b):
             res = sbuf(name, [P, t1 - t0, b - a], F32)
-            for t in range(t0, t1):
-                product(o_ps[:, t - t0, :], w2_q, w2_s, t, codes[:], scales[:])
-            nc.vector.scalar_tensor_tensor(res[:], y_keep[:, t0:t1, a:b], 1.5, o_ps[:], ALU.mult, ALU.add)
+            nc.vector.scalar_tensor_tensor(res[:], y_keep[:, t0:t1, a:b], 1.5, sums, ALU.mult, ALU.add)
             nc.sync.dma_start(out_rows[:, t0:t1, a:b], res[:])
 
-        e4 = sbuf("e4_first", [P, PACK, HALF], F32)
-        e3 = sbuf("e3_first", [P, PACK, HALF], F32, tag="e_shared")
-        r4 = sbuf("r4_first", [P, PACK, HALF], F32)
-        planes = sbuf("planes_first", [P, PACK, HALF], BF16)
-        for t in range(PACK):
-            differences(e4[:, t, :], n4_t, t, 0)
-        nc.scalar.activation(r4[:], e4[:], ACT.Relu, scale=-0.5)
-        for t in range(PACK):
-            differences(e3[:, t, :], n3_t, t, 0)
-        nc.vector.scalar_tensor_tensor(planes[:], e3[:], 0.0, r4[:], ALU.max, ALU.add)
-        codes, scales = quantise("z2_first", planes[:], HALF, nc.scalar.copy, tag="grouped_shared")
-        for r in range(2):
-            finish("res_first%d" % r, codes, scales, 4 * r, 2 * r, 2 * r + 2, 0, HALF)
+        planes = hinge("first", 0, "e4_then_y", "e3_then_e4")
+        grouped = interleave("first_b", planes[:], HALF, nc.scalar.copy, tag="grouped_then_e3")
+        sums_first = last_product("first", grouped, HALF, (0, 1))
+        y_keep = sbuf("y_keep", [P, PACK, S], F32, tag="e4_then_y")
+        nc.sync.dma_start(y_keep[:, 0, :], y_first[:])
+        for t in range(1, PACK):
+            nc.scalar.copy(y_keep[:, t, :], y_ps[t + 1][:])
 
-        e4 = sbuf("e4_second", [P, PACK, HALF], F32, tag="e_shared")
-        e3 = sbuf("e3_second", [P, PACK, HALF], F32, tag="grouped_shared")
-        r4 = sbuf("r4_second", [P, PACK, HALF], F32)
-        for t in range(PACK):
-            differences(e4[:, t, :], n4_t, t, 1)
-        nc.scalar.activation(r4[:], e4[:], ACT.Relu, scale=-0.5)
-        for t in range(PACK):
-            differences(e3[:, t, :], n3_t, t, 1)
-        packed = []
-        for v in range(2):
-            cols = slice(v * QUARTER, (v + 1) * QUARTER)
-            planes = sbuf("planes_second%d" % v, [P, PACK, QUARTER], BF16)
-            nc.vector.scalar_tensor_tensor(planes[:], e3[:, :, cols], 0.0, r4[:, :, cols], ALU.max, ALU.add)
-            interleave = nc.scalar.copy if v == 0 else nc.vector.tensor_copy
-            packed.append(quantise("z2_second%d" % v, planes[:], QUARTER, interleave))
-        for v in range(2):
-            a = HALF + v * QUARTER
-            finish("res_second%d" % v, packed[v][0], packed[v][1], 2 + 4 * v, 0, PACK, a, a + QUARTER)
+        planes = hinge("second", 1, "e3_then_e4", "grouped_then_e3")
+        third = interleave("third_b", planes[:, :, 0:QUARTER], QUARTER, nc.scalar.copy)
+        fourth = interleave("fourth_b", planes[:, :, QUARTER:HALF], QUARTER, nc.vector.tensor_copy)
+        sums_fourth = last_product("fourth", fourth, QUARTER, (5,))
+        sums_third = last_product("third", third, QUARTER, (6,))
+        for r in range(2):
+            finish("res_first%d" % r, sums_first[r][:], 2 * r, 2 * r + 2, 0, HALF)
+        finish("res_fourth", sums_fourth[0][:], 0, PACK, HALF + QUARTER, S)
+        for r in range(2):
+            finish("res_third%d" % r, sums_third[0][:, 2 * r : 2 * r + 2, :], 2 * r, 2 * r + 2, HALF, HALF + QUARTER)

@@ -41,7 +41,8 @@ def tile_picked_iterfoldhinge_none_p_kernel(
         n2_t = sbuf("n2_t", [P, W // 16], U16)
         n3_t = sbuf("n3_t", [P, S // 16], U16)
         n4_t = sbuf("n4_t", [P, S // 16], U16)
-        w1_raw = sbuf("w1_raw", [P, PACK, H], F32, tag="w_raw")
+        w1_raw = sbuf("w1_raw", [P, PACK, H], F32)
+        w2_raw = [sbuf("w2_raw%d" % r, [P, 2, H], F32) for r in range(2)]
         x_all = sbuf("x_all", [P, T], I32)
         xs_all = sbuf("xs_all", [P, T], U8)
         gain = sbuf("gain", [P, PACK], F32)
@@ -56,6 +57,8 @@ def tile_picked_iterfoldhinge_none_p_kernel(
         nc.sync.dma_start(x_all[:], x_words[0].rearrange("p n t -> p (n t)").bitcast(I32))
         nc.sync.dma_start(n1_t[:], n1)
         nc.sync.dma_start(n2_t[:], n2)
+        for r in range(2):
+            nc.sync.dma_start(w2_raw[r][:], w2.rearrange("(p j) c -> p j c", j=PACK)[:, 2 * r : 2 * r + 2, :])
         nc.sync.dma_start(n3_t[:], n3)
         nc.sync.dma_start(n4_t[:], n4)
         nc.vector.memset(warm_in[:], 0.0)
@@ -80,9 +83,6 @@ def tile_picked_iterfoldhinge_none_p_kernel(
         w1_q = sbuf("w1_q", [P, H], U32)
         w1_s = sbuf("w1_s", [P, H], U8)
         nc.vector.quantize_mx(out=w1_q[:].bitcast(FP8X4), scales=w1_s[:], in_=w1_b[:])
-
-        w2_raw = sbuf("w2_raw", [P, PACK, H], F32, tag="w_raw")
-        nc.sync.dma_start(w2_raw[:], w2.rearrange("(p j) c -> p j c", j=PACK))
 
         w1_tiles = [(w1_q[:, t * P : (t + 1) * P], w1_s[:, t * P : (t + 1) * P]) for t in range(PACK)]
         two = sbuf("two", [P, PACK], F32)
@@ -117,7 +117,8 @@ def tile_picked_iterfoldhinge_none_p_kernel(
         ds = [sbuf("ds%d" % t, [P, S], F32) for t in range(PACK)]
         w2_signed = sbuf("w2_signed", [P, PACK, H], BF16, tag="planes")
         w2_b = sbuf("w2_b", [P, PACK * H], BF16)
-        y_first = sbuf("y_first", [P, S], F32)
+        for j in range(2):
+            nc.vector.tensor_scalar(w2_signed[:, j, :], w2_raw[0][:, j, :], sign[:, j : j + 1], None, ALU.mult)
         gate = [sbuf("gate%d" % t, [P, W], F32) for t in range(PACK)]
         pa = [sbuf("pa%d" % t, [P, W], F32) for t in range(PACK)]
 
@@ -138,10 +139,8 @@ def tile_picked_iterfoldhinge_none_p_kernel(
             if t + 1 < PACK:
                 fetch(t + 1)
             fold(t)
-        for u in range(2):
-            nc.scalar.copy(y_first[:, halves[u]], y_ps[u][:])
-        for j in range(PACK):
-            nc.gpsimd.tensor_scalar(w2_signed[:, j, :], w2_raw[:, j, :], sign[:, j : j + 1], 0.0, ALU.mult, ALU.add)
+        for j in range(2, PACK):
+            nc.scalar.activation(w2_signed[:, j, :], w2_raw[1][:, j - 2, :], ACT.Copy, scale=sign[:, j : j + 1])
         deal(nc.scalar.copy, w2_b, w2_signed, 0, P)
         z_planes = sbuf("z_planes", [P, PACK, S], BF16, tag="planes")
         for t in range(PACK - 1):
@@ -172,14 +171,13 @@ def tile_picked_iterfoldhinge_none_p_kernel(
         nc.vector.quantize_mx(out=w2_q[:, P:].bitcast(FP8X4), scales=w2_s[:, P:], in_=w2_b[:, 2 * PACK * P :])
         w2_tiles = [(w2_q0[:], w2_s0[:])]
         w2_tiles.extend((w2_q[:, t * P : (t + 1) * P], w2_s[:, t * P : (t + 1) * P]) for t in range(PACK - 1))
-        h_banks = (0, 1, 5, 6, 7)
-        h_ps = [bank(i, [P, cols.stop - cols.start]) for i, (t, cols) in zip(h_banks, pieces)]
-        for (t, cols), ps in zip(pieces, h_ps):
-            product(ps[:], w2_tiles[t], z_q[:, cols], z_s[:, cols])
+        h_banks = (5, 6, 7, 5, 6)
 
         window = [sbuf("window%d" % t, [P, S], F32) for t in range(PACK)]
         plain = [[sbuf("plain%d_%d" % (t, u), [P, HALF], F32) for u in range(2)] for t in range(PACK)]
-        for (t, cols), ps in zip(pieces, h_ps):
+        for (t, cols), index in zip(pieces, h_banks):
+            ps = bank(index, [P, cols.stop - cols.start])
+            product(ps[:], w2_tiles[t], z_q[:, cols], z_s[:, cols])
             scale = neg_size[:, t : t + 1]
             nc.scalar.activation(window[t][:, cols], ps[:], ACT.Copy, scale=scale)
             if cols.start == 0 and t == 0:
@@ -236,17 +234,16 @@ def tile_picked_iterfoldhinge_none_p_kernel(
 
         planes = hinge("first", 0, "e4_then_y", "e3_then_e4")
         grouped = interleave("first_b", planes[:], HALF, nc.scalar.copy, tag="grouped_then_e3")
-        sums_first = last_product("first", grouped, HALF, (0, 1))
+        sums_first = last_product("first", grouped, HALF, (7, 5))
         y_keep = sbuf("y_keep", [P, PACK, S], F32, tag="e4_then_y")
-        nc.sync.dma_start(y_keep[:, 0, :], y_first[:])
-        for t in range(1, PACK):
-            nc.scalar.copy(y_keep[:, t, :], y_ps[t + 1][:])
+        for (t, cols), ps in zip(pieces, y_ps):
+            nc.scalar.copy(y_keep[:, t, cols], ps[:])
 
         planes = hinge("second", 1, "e3_then_e4", "grouped_then_e3")
         third = interleave("third_b", planes[:, :, 0:QUARTER], QUARTER, nc.scalar.copy)
         fourth = interleave("fourth_b", planes[:, :, QUARTER:HALF], QUARTER, nc.vector.tensor_copy)
-        sums_fourth = last_product("fourth", fourth, QUARTER, (5,))
-        sums_third = last_product("third", third, QUARTER, (6,))
+        sums_fourth = last_product("fourth", fourth, QUARTER, (6,))
+        sums_third = last_product("third", third, QUARTER, (0,))
         for r in range(2):
             finish("res_first%d" % r, sums_first[r][:], 2 * r, 2 * r + 2, 0, HALF)
         finish("res_fourth", sums_fourth[0][:], 0, PACK, HALF + QUARTER, S)

@@ -1,6 +1,7 @@
 from contextlib import ExitStack
 
 import concourse.mybir as mybir
+from concourse.masks import make_identity
 
 K, T, S, H, W = 512, 2048, 512, 512, 256
 FLOPS = 3 * 2 * 512 * 512 * 512
@@ -55,10 +56,11 @@ def tile_picked_iterfoldhinge_none_p_kernel(
         nc.sync.dma_start(offs_t[:], offs)
         nc.sync.dma_start(w1_raw[:], w1.rearrange("(p j) c -> p j c", j=PACK))
         nc.sync.dma_start(x_all[:], x_words[0].rearrange("p n t -> p (n t)").bitcast(I32))
+        w2_rows = w2.rearrange("(p j) c -> p j c", j=PACK)
+        nc.sync.dma_start(w2_raw[0][:], w2_rows[:, 0:2, :])
         nc.sync.dma_start(n1_t[:], n1)
         nc.sync.dma_start(n2_t[:], n2)
-        for r in range(2):
-            nc.sync.dma_start(w2_raw[r][:], w2.rearrange("(p j) c -> p j c", j=PACK)[:, 2 * r : 2 * r + 2, :])
+        nc.sync.dma_start(w2_raw[1][:], w2_rows[:, 2:4, :])
         nc.sync.dma_start(n3_t[:], n3)
         nc.sync.dma_start(n4_t[:], n4)
         nc.vector.memset(warm_in[:], 0.0)
@@ -73,8 +75,8 @@ def tile_picked_iterfoldhinge_none_p_kernel(
 
         def deal(engine_copy, grouped, rows, m0, m1):
             engine_copy(
-                grouped[:].rearrange("p (t m j) -> p m t j", t=PACK, j=PACK)[:, m0:m1],
-                rows[:].rearrange("p j (m t) -> p m t j", t=PACK)[:, m0:m1],
+                grouped[:].rearrange("p (t m j) -> p m j t", t=PACK, j=PACK)[:, m0:m1],
+                rows[:].rearrange("p j (m t) -> p m j t", t=PACK)[:, m0:m1],
             )
 
         w1_b = sbuf("w1_b", [P, PACK * H], BF16)
@@ -82,9 +84,19 @@ def tile_picked_iterfoldhinge_none_p_kernel(
         deal(nc.scalar.copy, w1_b, w1_raw, W1_VECTOR_M, P)
         w1_q = sbuf("w1_q", [P, H], U32)
         w1_s = sbuf("w1_s", [P, H], U8)
-        nc.vector.quantize_mx(out=w1_q[:].bitcast(FP8X4), scales=w1_s[:], in_=w1_b[:])
+
+        def quantise_tiles(codes, scales, grouped, t0, t1):
+            nc.vector.quantize_mx(out=codes.bitcast(FP8X4), scales=scales, in_=grouped[:, t0 * PACK * P : t1 * PACK * P])
+
+        quantise_tiles(w1_q[:, 0:P], w1_s[:, 0:P], w1_b, 0, 1)
 
         w1_tiles = [(w1_q[:, t * P : (t + 1) * P], w1_s[:, t * P : (t + 1) * P]) for t in range(PACK)]
+        ident = sbuf("ident", [P, P], F32)
+        make_identity(nc, ident[:])
+
+        def weave(copy, grouped, planes):
+            copy(grouped.rearrange("p (c i) t -> p c t i", i=PACK), planes.rearrange("p t (c i) -> p c t i", i=PACK))
+
         two = sbuf("two", [P, PACK], F32)
         sign = sbuf("sign", [P, PACK], F32)
         size = sbuf("size", [P, PACK], F32)
@@ -110,15 +122,19 @@ def tile_picked_iterfoldhinge_none_p_kernel(
         xq = sbuf("xq", [P, S], U32)
         for u in range(2):
             nc.vector.tensor_copy(xq[:, halves[u]], x_all[:].bitcast(U32).indirect(offs_t[:, u * 16 : (u + 1) * 16]))
+        quantise_tiles(w1_q[:, P : 2 * P], w1_s[:, P : 2 * P], w1_b, 1, 2)
+        quantise_tiles(w1_q[:, 2 * P :], w1_s[:, 2 * P :], w1_b, 2, 4)
         y_ps = [bank(i, [P, cols.stop - cols.start]) for i, (t, cols) in enumerate(pieces)]
         for (t, cols), ps in zip(pieces, y_ps):
             product(ps[:], w1_tiles[t], xq[:, cols], xs[:, cols])
 
         ds = [sbuf("ds%d" % t, [P, S], F32) for t in range(PACK)]
-        w2_signed = sbuf("w2_signed", [P, PACK, H], BF16, tag="planes")
+        planes_shared = sbuf("planes_shared", [P, PACK + 1, S], BF16)
+        w2_signed = planes_shared[:, 1 : PACK + 1, :]
         w2_b = sbuf("w2_b", [P, PACK * H], BF16)
         for j in range(2):
             nc.vector.tensor_scalar(w2_signed[:, j, :], w2_raw[0][:, j, :], sign[:, j : j + 1], None, ALU.mult)
+        y_keep = sbuf("y_keep", [P, PACK, S], F32)
         gate = [sbuf("gate%d" % t, [P, W], F32) for t in range(PACK)]
         pa = [sbuf("pa%d" % t, [P, W], F32) for t in range(PACK)]
 
@@ -126,6 +142,8 @@ def tile_picked_iterfoldhinge_none_p_kernel(
             for (tt, cols), ps in zip(pieces, y_ps):
                 if tt == t:
                     nc.scalar.copy(ds[t][:, cols], ps[:])
+            if t > 0:
+                nc.sync.dma_start(y_keep[:, t, :], ds[t][:])
             nc.vector.tensor_copy(pa[t][:], ds[t][:].indirect(n1_t[:]))
 
         def fold(t):
@@ -141,24 +159,24 @@ def tile_picked_iterfoldhinge_none_p_kernel(
             fold(t)
         for j in range(2, PACK):
             nc.scalar.activation(w2_signed[:, j, :], w2_raw[1][:, j - 2, :], ACT.Copy, scale=sign[:, j : j + 1])
-        deal(nc.scalar.copy, w2_b, w2_signed, 0, P)
-        z_planes = sbuf("z_planes", [P, PACK, S], BF16, tag="planes")
+        z_planes = planes_shared[:, 0:PACK, :]
         for t in range(PACK - 1):
             nc.scalar.activation(z_planes[:, t, :], ds[t][:], ACT.Copy, scale=size[:, t : t + 1])
+            if t == 0:
+                deal(nc.scalar.copy, w2_b, w2_signed, 0, P)
         t = PACK - 1
-        for u in range(2):
-            nc.scalar.activation(z_planes[:, t, halves[u]], ds[t][:, halves[u]], ACT.Copy, scale=size[:, t : t + 1])
+        nc.scalar.activation(z_planes[:, t, halves[1]], ds[t][:, halves[1]], ACT.Copy, scale=size[:, t : t + 1])
         w2_q0 = sbuf("w2_q0", [P, P], U32)
         w2_s0 = sbuf("w2_s0", [P, P], U8)
         nc.vector.quantize_mx(out=w2_q0[:].bitcast(FP8X4), scales=w2_s0[:], in_=w2_b[:, 0 : PACK * P])
+        nc.vector.tensor_scalar(z_planes[:, t, halves[0]], ds[t][:, halves[0]], size[:, t : t + 1], None, ALU.mult)
 
         z_b = [sbuf("z_b%d" % u, [P, HALF, PACK], BF16, tag="z_b%d" % u) for u in range(2)]
         z_q = sbuf("z_q", [P, S], U32)
         z_s = sbuf("z_s", [P, S], U8)
-        z_cols = z_planes[:].rearrange("p t c -> p c t")
-        nc.vector.tensor_copy(z_b[0][:], z_cols[:, halves[0]])
-        nc.scalar.copy(z_b[1][:, 0:QUARTER], z_cols[:, HALF : HALF + QUARTER])
-        nc.vector.tensor_copy(z_b[1][:, QUARTER:HALF], z_cols[:, HALF + QUARTER : S])
+        weave(nc.vector.tensor_copy, z_b[0][:], z_planes[:, :, halves[0]])
+        weave(nc.scalar.copy, z_b[1][:, 0:QUARTER, :], z_planes[:, :, HALF : HALF + QUARTER])
+        weave(nc.vector.tensor_copy, z_b[1][:, QUARTER:HALF, :], z_planes[:, :, HALF + QUARTER : S])
         for u in range(2):
             nc.vector.quantize_mx(
                 out=z_q[:, halves[u]].bitcast(FP8X4),
@@ -171,7 +189,7 @@ def tile_picked_iterfoldhinge_none_p_kernel(
         nc.vector.quantize_mx(out=w2_q[:, P:].bitcast(FP8X4), scales=w2_s[:, P:], in_=w2_b[:, 2 * PACK * P :])
         w2_tiles = [(w2_q0[:], w2_s0[:])]
         w2_tiles.extend((w2_q[:, t * P : (t + 1) * P], w2_s[:, t * P : (t + 1) * P]) for t in range(PACK - 1))
-        h_banks = (5, 6, 7, 5, 6)
+        h_banks = (5, 6, 7, 2, 3)
 
         window = [sbuf("window%d" % t, [P, S], F32) for t in range(PACK)]
         plain = [[sbuf("plain%d_%d" % (t, u), [P, HALF], F32) for u in range(2)] for t in range(PACK)]
@@ -186,6 +204,10 @@ def tile_picked_iterfoldhinge_none_p_kernel(
                 nc.scalar.activation(plain[t][0][:], ps[:, halves[0]], ACT.Copy, scale=scale)
             if cols.stop == S:
                 nc.sync.dma_start(plain[t][1][:], window[t][:, halves[1]])
+        y_first = sbuf("y_first", [P, S], F32, tag="planes_shared")
+        for u in range(2):
+            nc.scalar.copy(y_first[:, halves[u]], y_ps[u][:])
+        nc.sync.dma_start(y_keep[:, 0, :], y_first[:])
 
         out_rows = out.rearrange("(p t) s -> p t s", t=PACK)
         plane_groups = (slice(0, PACK - 1), slice(PACK - 1, PACK))
@@ -195,24 +217,25 @@ def tile_picked_iterfoldhinge_none_p_kernel(
                 dst, window[t][:].indirect(list_t[:, u * 16 : (u + 1) * 16]), plain[t][u][:], ALU.subtract
             )
 
-        def hinge(name, u, e4_tag, e3_tag):
-            e4 = sbuf(name + "_e4", [P, PACK, HALF], F32, tag=e4_tag)
-            e3 = sbuf(name + "_e3", [P, PACK, HALF], F32, tag=e3_tag)
-            r4 = sbuf(name + "_r4", [P, PACK, HALF], F32)
-            planes = sbuf(name + "_planes", [P, PACK, HALF], BF16)
+        def sum_on_tensor(name, r4, r3, blocks, sum_banks, word_bank, tag, rows_tag):
+            grouped = sbuf(name + "_b", [P, blocks * P, PACK], BF16, tag=tag)
+            sums = [bank(i, [P, PACK, P]) for i in sum_banks]
             for t in range(PACK):
-                differences(e4[:, t, :], n4_t, t, u)
-            for g in plane_groups:
-                nc.scalar.activation(r4[:, g, :], e4[:, g, :], ACT.Relu, scale=-0.5)
-            for t in range(PACK):
-                differences(e3[:, t, :], n3_t, t, u)
-            for g in plane_groups:
-                nc.vector.scalar_tensor_tensor(planes[:, g, :], e3[:, g, :], 0.0, r4[:, g, :], ALU.max, ALU.add)
-            return planes
-
-        def interleave(name, planes, n, copy, tag=None):
-            grouped = sbuf(name, [P, n, PACK], BF16, tag=tag)
-            copy(grouped[:], planes.rearrange("p t c -> p c t"))
+                for b in range(blocks):
+                    cols = slice(b * P, (b + 1) * P)
+                    nc.tensor.matmul(sums[b][:, t, :], r4[:, t, cols], ident[:], start=True, stop=False, is_transpose=True)
+                    nc.tensor.matmul(sums[b][:, t, :], r3[:, t, cols], ident[:], start=False, stop=True, is_transpose=True)
+            words = bank(word_bank, [P, blocks, 2, P])
+            rows = sbuf(name + "_rows", [P, blocks, 2, P, 2], BF16, tag=rows_tag)
+            for b in range(blocks):
+                nc.scalar.copy(rows[:, b], sums[b][:].rearrange("p (e r) m -> p e m r", r=2))
+                pairs = rows[:, b].rearrange("p e m r -> p (e m r)").bitcast(F32)
+                for e in range(2):
+                    nc.tensor.transpose(words[:, b, e, :], pairs[:, e * P : (e + 1) * P], ident[:])
+            nc.scalar.copy(
+                grouped[:].rearrange("p c t -> p (c t)").bitcast(F32).rearrange("p (b c e) -> p b c e", b=blocks, e=2),
+                words[:].rearrange("p b e c -> p b c e"),
+            )
             return grouped
 
         def last_product(name, grouped, n, banks):
@@ -232,20 +255,38 @@ def tile_picked_iterfoldhinge_none_p_kernel(
             nc.vector.scalar_tensor_tensor(res[:], y_keep[:, t0:t1, a:b], 1.5, sums, ALU.mult, ALU.add)
             nc.sync.dma_start(out_rows[:, t0:t1, a:b], res[:])
 
-        planes = hinge("first", 0, "e4_then_y", "e3_then_e4")
-        grouped = interleave("first_b", planes[:], HALF, nc.scalar.copy, tag="grouped_then_e3")
-        sums_first = last_product("first", grouped, HALF, (7, 5))
-        y_keep = sbuf("y_keep", [P, PACK, S], F32, tag="e4_then_y")
-        for (t, cols), ps in zip(pieces, y_ps):
-            nc.scalar.copy(y_keep[:, t, cols], ps[:])
+        e4 = sbuf("first_e4", [P, PACK, HALF], F32)
+        e3 = sbuf("first_e3", [P, PACK, HALF], F32)
+        r4 = sbuf("first_r4", [P, PACK, HALF], F32)
+        r3 = sbuf("first_r3", [P, PACK, HALF], F32)
+        for t in range(PACK):
+            differences(e4[:, t, :], n4_t, t, 0)
+            differences(e3[:, t, :], n3_t, t, 0)
+        for g in (slice(0, 2), slice(2, 3), slice(3, 4)):
+            nc.scalar.activation(r4[:, g, :], e4[:, g, :], ACT.Relu, scale=-0.5)
+            nc.scalar.activation(r3[:, g, :], e3[:, g, :], ACT.Relu)
+        grouped = sum_on_tensor("first", r4, r3, 2, (4, 5), 7, None, "rows_then_relu")
+        sums_first = last_product("first", grouped, HALF, (3, 4))
 
-        planes = hinge("second", 1, "e3_then_e4", "grouped_then_e3")
-        third = interleave("third_b", planes[:, :, 0:QUARTER], QUARTER, nc.scalar.copy)
-        fourth = interleave("fourth_b", planes[:, :, QUARTER:HALF], QUARTER, nc.vector.tensor_copy)
-        sums_fourth = last_product("fourth", fourth, QUARTER, (6,))
-        sums_third = last_product("third", third, QUARTER, (0,))
+        e4 = sbuf("second_e4", [P, PACK, HALF], F32, tag="plain3_0")
+        e3 = sbuf("second_e3", [P, PACK, HALF], F32, tag="first_e4")
+        r4 = sbuf("second_r4", [P, PACK, HALF], F32, tag="rows_then_relu")
+        planes = sbuf("second_planes", [P, PACK, HALF], BF16)
+        for t in range(PACK):
+            differences(e4[:, t, :], n4_t, t, 1)
+        nc.scalar.activation(r4[:], e4[:], ACT.Relu, scale=-0.5)
+        for t in range(PACK):
+            differences(e3[:, t, :], n3_t, t, 1)
+        nc.vector.scalar_tensor_tensor(planes[:], e3[:], 0.0, r4[:], ALU.max, ALU.add)
+        third = sbuf("third_b", [P, QUARTER, PACK], BF16)
+        fourth = sbuf("fourth_b", [P, QUARTER, PACK], BF16)
+        weave(nc.scalar.copy, third[:], planes[:, :, 0:QUARTER])
+        weave(nc.vector.tensor_copy, fourth[:], planes[:, :, QUARTER:HALF])
+        sums_fourth = last_product("fourth", fourth, QUARTER, (5, 7))
+        sums_third = last_product("third", third, QUARTER, (0, 1))
         for r in range(2):
             finish("res_first%d" % r, sums_first[r][:], 2 * r, 2 * r + 2, 0, HALF)
-        finish("res_fourth", sums_fourth[0][:], 0, PACK, HALF + QUARTER, S)
         for r in range(2):
-            finish("res_third%d" % r, sums_third[0][:, 2 * r : 2 * r + 2, :], 2 * r, 2 * r + 2, HALF, HALF + QUARTER)
+            finish("res_fourth%d" % r, sums_fourth[r][:], 2 * r, 2 * r + 2, HALF + QUARTER, S)
+        for r in range(2):
+            finish("res_third%d" % r, sums_third[r][:], 2 * r, 2 * r + 2, HALF, HALF + QUARTER)

@@ -3,7 +3,7 @@ from contextlib import ExitStack
 import concourse.mybir as mybir
 from concourse.masks import make_identity
 
-K, T, S, H, W = 512, 2048, 512, 512, 256
+T, S, H, W = 2048, 512, 512, 256
 FLOPS = 3 * 2 * 512 * 512 * 512
 
 F32 = mybir.dt.float32
@@ -18,9 +18,11 @@ ACT = mybir.ActivationFunctionType
 
 P = 128
 PACK = 4
+GROUP = 16
+QUADRANT = 32
 HALF = S // 2
 QUARTER = S // 4
-W1_VECTOR_M = 64
+STEEP = 2.0**100
 
 
 def tile_picked_iterfoldhinge_none_p_kernel(
@@ -37,25 +39,51 @@ def tile_picked_iterfoldhinge_none_p_kernel(
         def bank(index, shape):
             return psum.tile(shape, F32, name="bank%d" % index)
 
-        offs_t = sbuf("offs_t", [P, S // 16], U16)
-        n1_t = sbuf("n1_t", [P, W // 16], U16)
-        n2_t = sbuf("n2_t", [P, W // 16], U16)
-        n3_t = sbuf("n3_t", [P, S // 16], U16)
-        n4_t = sbuf("n4_t", [P, S // 16], U16)
+        def deal(copy, dealt, rows):
+            copy(
+                dealt[:].rearrange("p (t m j) -> p m j t", t=PACK, j=PACK),
+                rows[:].rearrange("p j (m t) -> p m j t", t=PACK),
+            )
+
+        def weave(copy, woven, planes):
+            copy(woven.rearrange("p (c i) t -> p c t i", i=PACK), planes.rearrange("p t (c i) -> p c t i", i=PACK))
+
+        def quantise_weights(codes, scales, dealt, t0, t1):
+            nc.vector.quantize_mx(out=codes.bitcast(FP8X4), scales=scales, in_=dealt[:, t0 * PACK * P : t1 * PACK * P])
+
+        def quantise_woven(codes, scales, woven):
+            nc.vector.quantize_mx(out=codes.bitcast(FP8X4), scales=scales, in_=woven[:].rearrange("p c t -> p (c t)"))
+
+        def product(dst, weights, codes, scales):
+            nc.tensor.matmul_mx(
+                out=dst,
+                lhsT=weights[0].bitcast(FP8X4),
+                lhsT_scale=weights[1],
+                rhs=codes.bitcast(FP8X4),
+                rhs_scale=scales,
+                start=True,
+                stop=True,
+            )
+
+        offs_t = sbuf("offs_t", [P, S // GROUP], U16)
+        n1_t = sbuf("n1_t", [P, W // GROUP], U16)
+        n2_t = sbuf("n2_t", [P, W // GROUP], U16)
+        n3_t = sbuf("n3_t", [P, S // GROUP], U16)
+        n4_t = sbuf("n4_t", [P, S // GROUP], U16)
         w1_raw = sbuf("w1_raw", [P, PACK, H], F32)
         w2_raw = [sbuf("w2_raw%d" % r, [P, 2, H], F32) for r in range(2)]
         x_all = sbuf("x_all", [P, T], I32)
         xs_all = sbuf("xs_all", [P, T], U8)
         gain = sbuf("gain", [P, PACK], F32)
-        warm_in = sbuf("warm_in", [P, 1], F32)
-        warm_out = sbuf("warm_out", [P, 1], F32)
 
         xs_rows = sbuf("xs_rows", [P, T // 4], I32)
-        for q in range(4):
-            nc.sync.dma_start(xs_rows[32 * q : 32 * q + 4, :], x_scales[0, 4 * q : 4 * q + 4, :].bitcast(I32))
+        live = [slice(QUADRANT * q, QUADRANT * q + 4) for q in range(P // QUADRANT)]
+        for q, rows in enumerate(live):
+            nc.sync.dma_start(xs_rows[rows, :], x_scales[0, 4 * q : 4 * q + 4, :].bitcast(I32))
         nc.sync.dma_start(offs_t[:], offs)
         nc.sync.dma_start(w1_raw[:], w1.rearrange("(p j) c -> p j c", j=PACK))
         nc.sync.dma_start(x_all[:], x_words[0].rearrange("p n t -> p (n t)").bitcast(I32))
+        nc.sync.dma_start(gain[:], gn.rearrange("(p t) o -> p (t o)", t=PACK))
         w2_rows = w2.rearrange("(p j) c -> p j c", j=PACK)
         nc.sync.dma_start(w2_raw[0][:], w2_rows[:, 0:2, :])
         nc.sync.dma_start(n1_t[:], n1)
@@ -63,75 +91,49 @@ def tile_picked_iterfoldhinge_none_p_kernel(
         nc.sync.dma_start(w2_raw[1][:], w2_rows[:, 2:4, :])
         nc.sync.dma_start(n3_t[:], n3)
         nc.sync.dma_start(n4_t[:], n4)
-        nc.vector.memset(warm_in[:], 0.0)
         nc.vector.memset(xs_all[:].bitcast(I32), 0)
-        for q in range(4):
-            nc.vector.tensor_copy(xs_all[32 * q : 32 * q + 4, :].bitcast(I32), xs_rows[32 * q : 32 * q + 4, :])
-        nc.scalar.activation(warm_out[:], warm_in[:], ACT.Sigmoid)
-        nc.gpsimd.dma_start(gain[:], gn.rearrange("(p t) o -> p (t o)", t=PACK))
+        for rows in live:
+            nc.vector.tensor_copy(xs_all[rows, :].bitcast(I32), xs_rows[rows, :])
 
         xs = sbuf("xs", [P, S], U8)
         nc.vector.tensor_copy(xs[:], xs_all[:].indirect(offs_t[:]))
-
-        def deal(engine_copy, grouped, rows, m0, m1):
-            engine_copy(
-                grouped[:].rearrange("p (t m j) -> p m j t", t=PACK, j=PACK)[:, m0:m1],
-                rows[:].rearrange("p j (m t) -> p m j t", t=PACK)[:, m0:m1],
-            )
-
-        w1_b = sbuf("w1_b", [P, PACK * H], BF16)
-        deal(nc.vector.tensor_copy, w1_b, w1_raw, 0, W1_VECTOR_M)
-        deal(nc.scalar.copy, w1_b, w1_raw, W1_VECTOR_M, P)
+        w1_dealt = sbuf("w1_dealt", [P, PACK * H], BF16)
+        deal(nc.vector.tensor_copy, w1_dealt, w1_raw)
         w1_q = sbuf("w1_q", [P, H], U32)
         w1_s = sbuf("w1_s", [P, H], U8)
-
-        def quantise_tiles(codes, scales, grouped, t0, t1):
-            nc.vector.quantize_mx(out=codes.bitcast(FP8X4), scales=scales, in_=grouped[:, t0 * PACK * P : t1 * PACK * P])
-
-        quantise_tiles(w1_q[:, 0:P], w1_s[:, 0:P], w1_b, 0, 1)
-
+        quantise_weights(w1_q[:, 0:P], w1_s[:, 0:P], w1_dealt, 0, 1)
         w1_tiles = [(w1_q[:, t * P : (t + 1) * P], w1_s[:, t * P : (t + 1) * P]) for t in range(PACK)]
         ident = sbuf("ident", [P, P], F32)
         make_identity(nc, ident[:])
 
-        def weave(copy, grouped, planes):
-            copy(grouped.rearrange("p (c i) t -> p c t i", i=PACK), planes.rearrange("p t (c i) -> p c t i", i=PACK))
-
-        two = sbuf("two", [P, PACK], F32)
+        twice_step = sbuf("twice_step", [P, PACK], F32)
         sign = sbuf("sign", [P, PACK], F32)
         size = sbuf("size", [P, PACK], F32)
         neg_size = sbuf("neg_size", [P, PACK], F32)
-        nc.gpsimd.tensor_scalar(two[:], gain[:], 0.0, 2.0, ALU.is_ge, ALU.mult)
-        nc.gpsimd.tensor_scalar(sign[:], two[:], 1.0, -1.0, ALU.mult, ALU.add)
+        soft_step = sbuf("soft_step", [P, PACK], F32)
+        nc.scalar.activation(soft_step[:], gain[:], ACT.Sigmoid, scale=STEEP)
+        nc.gpsimd.tensor_scalar(twice_step[:], soft_step[:], 0.5, 2.0, ALU.is_ge, ALU.mult)
+        nc.gpsimd.tensor_scalar(sign[:], twice_step[:], 1.0, -1.0, ALU.mult, ALU.add)
         nc.gpsimd.tensor_tensor(size[:], gain[:], sign[:], ALU.mult)
         nc.gpsimd.tensor_scalar(neg_size[:], size[:], -1.0, 0.0, ALU.mult, ALU.add)
 
-        def product(dst, weights, rq, rs):
-            nc.tensor.matmul_mx(
-                out=dst,
-                lhsT=weights[0].bitcast(FP8X4),
-                lhsT_scale=weights[1],
-                rhs=rq.bitcast(FP8X4),
-                rhs_scale=rs,
-                start=True,
-                stop=True,
-            )
-
         halves = [slice(u * HALF, (u + 1) * HALF) for u in range(2)]
+        half_lists = [slice(u * HALF // GROUP, (u + 1) * HALF // GROUP) for u in range(2)]
         pieces = [(0, halves[0]), (0, halves[1])] + [(t, slice(0, S)) for t in range(1, PACK)]
         xq = sbuf("xq", [P, S], U32)
         for u in range(2):
-            nc.vector.tensor_copy(xq[:, halves[u]], x_all[:].bitcast(U32).indirect(offs_t[:, u * 16 : (u + 1) * 16]))
-        quantise_tiles(w1_q[:, P : 2 * P], w1_s[:, P : 2 * P], w1_b, 1, 2)
-        quantise_tiles(w1_q[:, 2 * P :], w1_s[:, 2 * P :], w1_b, 2, 4)
+            nc.vector.tensor_copy(xq[:, halves[u]], x_all[:].bitcast(U32).indirect(offs_t[:, half_lists[u]]))
+        quantise_weights(w1_q[:, P : 2 * P], w1_s[:, P : 2 * P], w1_dealt, 1, 2)
+        quantise_weights(w1_q[:, 2 * P :], w1_s[:, 2 * P :], w1_dealt, 2, PACK)
         y_ps = [bank(i, [P, cols.stop - cols.start]) for i, (t, cols) in enumerate(pieces)]
         for (t, cols), ps in zip(pieces, y_ps):
             product(ps[:], w1_tiles[t], xq[:, cols], xs[:, cols])
 
         ds = [sbuf("ds%d" % t, [P, S], F32) for t in range(PACK)]
-        planes_shared = sbuf("planes_shared", [P, PACK + 1, S], BF16)
-        w2_signed = planes_shared[:, 1 : PACK + 1, :]
-        w2_b = sbuf("w2_b", [P, PACK * H], BF16)
+        slots = sbuf("slots", [P, PACK + 1, S], BF16)
+        w2_signed = slots[:, 1 : PACK + 1, :]
+        z_planes = slots[:, 0:PACK, :]
+        w2_dealt = sbuf("w2_dealt", [P, PACK * H], BF16)
         for j in range(2):
             nc.vector.tensor_scalar(w2_signed[:, j, :], w2_raw[0][:, j, :], sign[:, j : j + 1], None, ALU.mult)
         y_keep = sbuf("y_keep", [P, PACK, S], F32)
@@ -139,8 +141,8 @@ def tile_picked_iterfoldhinge_none_p_kernel(
         pa = [sbuf("pa%d" % t, [P, W], F32) for t in range(PACK)]
 
         def fetch(t):
-            for (tt, cols), ps in zip(pieces, y_ps):
-                if tt == t:
+            for (plane, cols), ps in zip(pieces, y_ps):
+                if plane == t:
                     nc.scalar.copy(ds[t][:, cols], ps[:])
             if t > 0:
                 nc.sync.dma_start(y_keep[:, t, :], ds[t][:])
@@ -159,38 +161,35 @@ def tile_picked_iterfoldhinge_none_p_kernel(
             fold(t)
         for j in range(2, PACK):
             nc.scalar.activation(w2_signed[:, j, :], w2_raw[1][:, j - 2, :], ACT.Copy, scale=sign[:, j : j + 1])
-        z_planes = planes_shared[:, 0:PACK, :]
-        for t in range(PACK - 1):
+
+        last = PACK - 1
+        for t in range(last):
             nc.scalar.activation(z_planes[:, t, :], ds[t][:], ACT.Copy, scale=size[:, t : t + 1])
             if t == 0:
-                deal(nc.scalar.copy, w2_b, w2_signed, 0, P)
-        t = PACK - 1
-        nc.scalar.activation(z_planes[:, t, halves[1]], ds[t][:, halves[1]], ACT.Copy, scale=size[:, t : t + 1])
+                deal(nc.scalar.copy, w2_dealt, w2_signed)
+        last_size = size[:, last:PACK]
+        nc.scalar.activation(z_planes[:, last, halves[1]], ds[last][:, halves[1]], ACT.Copy, scale=last_size)
         w2_q0 = sbuf("w2_q0", [P, P], U32)
         w2_s0 = sbuf("w2_s0", [P, P], U8)
-        nc.vector.quantize_mx(out=w2_q0[:].bitcast(FP8X4), scales=w2_s0[:], in_=w2_b[:, 0 : PACK * P])
-        nc.vector.tensor_scalar(z_planes[:, t, halves[0]], ds[t][:, halves[0]], size[:, t : t + 1], None, ALU.mult)
+        quantise_weights(w2_q0[:], w2_s0[:], w2_dealt, 0, 1)
+        nc.vector.tensor_scalar(z_planes[:, last, halves[0]], ds[last][:, halves[0]], last_size, None, ALU.mult)
 
-        z_b = [sbuf("z_b%d" % u, [P, HALF, PACK], BF16, tag="z_b%d" % u) for u in range(2)]
+        z_woven = [sbuf("z_woven%d" % u, [P, HALF, PACK], BF16) for u in range(2)]
         z_q = sbuf("z_q", [P, S], U32)
         z_s = sbuf("z_s", [P, S], U8)
-        weave(nc.vector.tensor_copy, z_b[0][:], z_planes[:, :, halves[0]])
-        weave(nc.scalar.copy, z_b[1][:, 0:QUARTER, :], z_planes[:, :, HALF : HALF + QUARTER])
-        weave(nc.vector.tensor_copy, z_b[1][:, QUARTER:HALF, :], z_planes[:, :, HALF + QUARTER : S])
+        weave(nc.vector.tensor_copy, z_woven[0][:], z_planes[:, :, halves[0]])
+        weave(nc.scalar.copy, z_woven[1][:, 0:QUARTER, :], z_planes[:, :, HALF : HALF + QUARTER])
+        weave(nc.vector.tensor_copy, z_woven[1][:, QUARTER:HALF, :], z_planes[:, :, HALF + QUARTER : S])
         for u in range(2):
-            nc.vector.quantize_mx(
-                out=z_q[:, halves[u]].bitcast(FP8X4),
-                scales=z_s[:, halves[u]],
-                in_=z_b[u][:].rearrange("p c t -> p (c t)"),
-            )
-        w2_q = sbuf("w2_q", [P, H - P], U32, tag="z_b1")
+            quantise_woven(z_q[:, halves[u]], z_s[:, halves[u]], z_woven[u])
+        w2_q = sbuf("w2_q", [P, H - P], U32, tag="z_woven1")
         w2_s = sbuf("w2_s", [P, H - P], U8)
-        nc.vector.quantize_mx(out=w2_q[:, 0:P].bitcast(FP8X4), scales=w2_s[:, 0:P], in_=w2_b[:, PACK * P : 2 * PACK * P])
-        nc.vector.quantize_mx(out=w2_q[:, P:].bitcast(FP8X4), scales=w2_s[:, P:], in_=w2_b[:, 2 * PACK * P :])
+        quantise_weights(w2_q[:, 0:P], w2_s[:, 0:P], w2_dealt, 1, 2)
+        quantise_weights(w2_q[:, P:], w2_s[:, P:], w2_dealt, 2, PACK)
         w2_tiles = [(w2_q0[:], w2_s0[:])]
         w2_tiles.extend((w2_q[:, t * P : (t + 1) * P], w2_s[:, t * P : (t + 1) * P]) for t in range(PACK - 1))
-        h_banks = (5, 6, 7, 2, 3)
 
+        h_banks = (5, 6, 7, 2, 3)
         window = [sbuf("window%d" % t, [P, S], F32) for t in range(PACK)]
         plain = [[sbuf("plain%d_%d" % (t, u), [P, HALF], F32) for u in range(2)] for t in range(PACK)]
         for (t, cols), index in zip(pieces, h_banks):
@@ -204,89 +203,83 @@ def tile_picked_iterfoldhinge_none_p_kernel(
                 nc.scalar.activation(plain[t][0][:], ps[:, halves[0]], ACT.Copy, scale=scale)
             if cols.stop == S:
                 nc.sync.dma_start(plain[t][1][:], window[t][:, halves[1]])
-        y_first = sbuf("y_first", [P, S], F32, tag="planes_shared")
+        y_plane0 = sbuf("y_plane0", [P, S], F32, tag="slots")
         for u in range(2):
-            nc.scalar.copy(y_first[:, halves[u]], y_ps[u][:])
-        nc.sync.dma_start(y_keep[:, 0, :], y_first[:])
+            nc.scalar.copy(y_plane0[:, halves[u]], y_ps[u][:])
+        nc.sync.dma_start(y_keep[:, 0, :], y_plane0[:])
 
-        out_rows = out.rearrange("(p t) s -> p t s", t=PACK)
-        plane_groups = (slice(0, PACK - 1), slice(PACK - 1, PACK))
+        out_planes = out.rearrange("(p t) s -> p t s", t=PACK)
+        pairs = [slice(2 * r, 2 * r + 2) for r in range(2)]
 
         def differences(dst, list_t, t, u):
-            nc.vector.tensor_tensor(
-                dst, window[t][:].indirect(list_t[:, u * 16 : (u + 1) * 16]), plain[t][u][:], ALU.subtract
-            )
+            nc.vector.tensor_tensor(dst, window[t][:].indirect(list_t[:, half_lists[u]]), plain[t][u][:], ALU.subtract)
 
-        def sum_on_tensor(name, r4, r3, blocks, sum_banks, word_bank, tag, rows_tag):
-            grouped = sbuf(name + "_b", [P, blocks * P, PACK], BF16, tag=tag)
-            sums = [bank(i, [P, PACK, P]) for i in sum_banks]
-            for t in range(PACK):
-                for b in range(blocks):
-                    cols = slice(b * P, (b + 1) * P)
-                    nc.tensor.matmul(sums[b][:, t, :], r4[:, t, cols], ident[:], start=True, stop=False, is_transpose=True)
-                    nc.tensor.matmul(sums[b][:, t, :], r3[:, t, cols], ident[:], start=False, stop=True, is_transpose=True)
-            words = bank(word_bank, [P, blocks, 2, P])
-            rows = sbuf(name + "_rows", [P, blocks, 2, P, 2], BF16, tag=rows_tag)
-            for b in range(blocks):
-                nc.scalar.copy(rows[:, b], sums[b][:].rearrange("p (e r) m -> p e m r", r=2))
-                pairs = rows[:, b].rearrange("p e m r -> p (e m r)").bitcast(F32)
-                for e in range(2):
-                    nc.tensor.transpose(words[:, b, e, :], pairs[:, e * P : (e + 1) * P], ident[:])
-            nc.scalar.copy(
-                grouped[:].rearrange("p c t -> p (c t)").bitcast(F32).rearrange("p (b c e) -> p b c e", b=blocks, e=2),
-                words[:].rearrange("p b e c -> p b c e"),
-            )
-            return grouped
-
-        def last_product(name, grouped, n, banks):
+        def last_product(name, woven, n, banks):
             codes = sbuf(name + "_q", [P, n], U32)
             scales = sbuf(name + "_s", [P, n], U8)
-            nc.vector.quantize_mx(
-                out=codes[:].bitcast(FP8X4), scales=scales[:], in_=grouped[:].rearrange("p c t -> p (c t)")
-            )
-            per_bank = PACK // len(banks)
-            sums = [bank(i, [P, per_bank, n]) for i in banks]
+            quantise_woven(codes[:], scales[:], woven)
+            sums = [bank(i, [P, 2, n]) for i in banks]
             for t in range(PACK):
-                product(sums[t // per_bank][:, t % per_bank, :], w2_tiles[t], codes[:], scales[:])
+                product(sums[t // 2][:, t % 2, :], w2_tiles[t], codes[:], scales[:])
             return sums
 
-        def finish(name, sums, t0, t1, a, b):
-            res = sbuf(name, [P, t1 - t0, b - a], F32)
-            nc.vector.scalar_tensor_tensor(res[:], y_keep[:, t0:t1, a:b], 1.5, sums, ALU.mult, ALU.add)
-            nc.sync.dma_start(out_rows[:, t0:t1, a:b], res[:])
+        def finish(name, sums, a, b, tag=None):
+            res = sbuf(name, [P, PACK, b - a], F32, tag=tag)
+            for pair, ps in zip(pairs, sums):
+                nc.vector.scalar_tensor_tensor(res[:, pair, :], y_keep[:, pair, a:b], 1.5, ps[:], ALU.mult, ALU.add)
+                nc.sync.dma_start(out_planes[:, pair, a:b], res[:, pair, :])
 
-        e4 = sbuf("first_e4", [P, PACK, HALF], F32)
-        e3 = sbuf("first_e3", [P, PACK, HALF], F32)
-        r4 = sbuf("first_r4", [P, PACK, HALF], F32)
-        r3 = sbuf("first_r3", [P, PACK, HALF], F32)
+        d4_first = sbuf("d4_first", [P, PACK, HALF], F32)
+        d3_first = sbuf("d3_first", [P, PACK, HALF], F32)
+        r4_first = sbuf("r4_first", [P, PACK, HALF], F32)
+        r3_first = sbuf("r3_first", [P, PACK, HALF], F32)
         for t in range(PACK):
-            differences(e4[:, t, :], n4_t, t, 0)
-            differences(e3[:, t, :], n3_t, t, 0)
-        for g in (slice(0, 2), slice(2, 3), slice(3, 4)):
-            nc.scalar.activation(r4[:, g, :], e4[:, g, :], ACT.Relu, scale=-0.5)
-            nc.scalar.activation(r3[:, g, :], e3[:, g, :], ACT.Relu)
-        grouped = sum_on_tensor("first", r4, r3, 2, (4, 5), 7, None, "rows_then_relu")
-        sums_first = last_product("first", grouped, HALF, (3, 4))
+            differences(d4_first[:, t, :], n4_t, t, 0)
+            differences(d3_first[:, t, :], n3_t, t, 0)
+        for some in (pairs[0], slice(2, last), slice(last, PACK)):
+            nc.scalar.activation(r4_first[:, some, :], d4_first[:, some, :], ACT.Relu, scale=-0.5)
+            nc.scalar.activation(r3_first[:, some, :], d3_first[:, some, :], ACT.Relu)
 
-        e4 = sbuf("second_e4", [P, PACK, HALF], F32, tag="plain3_0")
-        e3 = sbuf("second_e3", [P, PACK, HALF], F32, tag="first_e4")
-        r4 = sbuf("second_r4", [P, PACK, HALF], F32, tag="rows_then_relu")
-        planes = sbuf("second_planes", [P, PACK, HALF], BF16)
+        blocks = HALF // P
+        first_woven = sbuf("first_woven", [P, HALF, PACK], BF16)
+        by_column = [bank(i, [P, PACK, P]) for i in (4, 5)]
         for t in range(PACK):
-            differences(e4[:, t, :], n4_t, t, 1)
-        nc.scalar.activation(r4[:], e4[:], ACT.Relu, scale=-0.5)
+            for b in range(blocks):
+                cols = slice(b * P, (b + 1) * P)
+                dst = by_column[b][:, t, :]
+                nc.tensor.matmul(dst, r4_first[:, t, cols], ident[:], start=True, stop=False, is_transpose=True)
+                nc.tensor.matmul(dst, r3_first[:, t, cols], ident[:], start=False, stop=True, is_transpose=True)
+        words = bank(7, [P, blocks, 2, P])
+        rounded = sbuf("rounded", [P, blocks, 2, P, 2], BF16)
+        for b in range(blocks):
+            nc.scalar.copy(rounded[:, b], by_column[b][:].rearrange("p (e r) m -> p e m r", r=2))
+            as_words = rounded[:, b].rearrange("p e m r -> p (e m r)").bitcast(F32)
+            for e in range(2):
+                nc.tensor.transpose(words[:, b, e, :], as_words[:, e * P : (e + 1) * P], ident[:])
+        nc.scalar.copy(
+            first_woven[:].rearrange("p c t -> p (c t)").bitcast(F32).rearrange("p (b c e) -> p b c e", b=blocks, e=2),
+            words[:].rearrange("p b e c -> p b c e"),
+        )
+        sums_first = last_product("first", first_woven, HALF, (3, 4))
+
+        d4_second = sbuf("d4_second", [P, PACK, HALF], F32, tag="plain3_0")
+        d3_second = sbuf("d3_second", [P, PACK, HALF], F32, tag="d4_first")
+        r4_second = [sbuf("r4_second0", [P, 2, HALF], F32), sbuf("r4_second1", [P, 2, HALF], F32, tag="rounded")]
+        z2_planes = sbuf("z2_planes", [P, PACK, HALF], BF16)
         for t in range(PACK):
-            differences(e3[:, t, :], n3_t, t, 1)
-        nc.vector.scalar_tensor_tensor(planes[:], e3[:], 0.0, r4[:], ALU.max, ALU.add)
-        third = sbuf("third_b", [P, QUARTER, PACK], BF16)
-        fourth = sbuf("fourth_b", [P, QUARTER, PACK], BF16)
-        weave(nc.scalar.copy, third[:], planes[:, :, 0:QUARTER])
-        weave(nc.vector.tensor_copy, fourth[:], planes[:, :, QUARTER:HALF])
-        sums_fourth = last_product("fourth", fourth, QUARTER, (5, 7))
-        sums_third = last_product("third", third, QUARTER, (0, 1))
-        for r in range(2):
-            finish("res_first%d" % r, sums_first[r][:], 2 * r, 2 * r + 2, 0, HALF)
-        for r in range(2):
-            finish("res_fourth%d" % r, sums_fourth[r][:], 2 * r, 2 * r + 2, HALF + QUARTER, S)
-        for r in range(2):
-            finish("res_third%d" % r, sums_third[r][:], 2 * r, 2 * r + 2, HALF, HALF + QUARTER)
+            differences(d4_second[:, t, :], n4_t, t, 1)
+        for pair, r4 in zip(pairs, r4_second):
+            nc.scalar.activation(r4[:], d4_second[:, pair, :], ACT.Relu, scale=-0.5)
+        for t in range(PACK):
+            differences(d3_second[:, t, :], n3_t, t, 1)
+        for pair, r4 in zip(pairs, r4_second):
+            nc.vector.scalar_tensor_tensor(z2_planes[:, pair, :], d3_second[:, pair, :], 0.0, r4[:], ALU.max, ALU.add)
+        third_woven = sbuf("third_woven", [P, QUARTER, PACK], BF16)
+        fourth_woven = sbuf("fourth_woven", [P, QUARTER, PACK], BF16)
+        weave(nc.scalar.copy, third_woven[:], z2_planes[:, :, 0:QUARTER])
+        weave(nc.vector.tensor_copy, fourth_woven[:], z2_planes[:, :, QUARTER:HALF])
+        sums_fourth = last_product("fourth", fourth_woven, QUARTER, (5, 7))
+        sums_third = last_product("third", third_woven, QUARTER, (0, 1))
+        finish("res_first", sums_first, 0, HALF, tag="plain3_0")
+        finish("res_fourth", sums_fourth, HALF + QUARTER, S)
+        finish("res_third", sums_third, HALF, HALF + QUARTER)

from contextlib import ExitStack

import concourse.mybir as mybir
from concourse.masks import make_identity

T, S, H, W = 2048, 512, 512, 256
FLOPS = 3 * 2 * 512 * 512 * 512

F32 = mybir.dt.float32
BF16 = mybir.dt.bfloat16
I32 = mybir.dt.int32
U32 = mybir.dt.uint32
U16 = mybir.dt.uint16
U8 = mybir.dt.uint8
FP8X4 = mybir.dt.float8_e4m3fn_x4
ALU = mybir.AluOpType
ACT = mybir.ActivationFunctionType

P = 128
PACK = 4
GROUP = 16
QUADRANT = 32
HALF = S // 2
QUARTER = S // 4
STEEP = 2.0**100


def tile_picked_iterfoldhinge_none_p_kernel(
    tc, x_words, x_scales, w1, gn, w2, offs, n1, n2, n3, n4, out
):
    nc = tc.nc
    with ExitStack() as ctx:
        keep = ctx.enter_context(tc.tile_pool(name="keep", bufs=1))
        psum = ctx.enter_context(tc.psum_pool(name="psum", bufs=1))

        def sbuf(name, shape, dtype, tag=None):
            return keep.tile(shape, dtype, name=name, tag=tag or name, align_bytes=64)

        def bank(index, shape):
            return psum.tile(shape, F32, name="bank%d" % index)

        def deal(copy, dealt, rows):
            copy(
                dealt[:].rearrange("p (t m j) -> p m j t", t=PACK, j=PACK),
                rows[:].rearrange("p j (m t) -> p m j t", t=PACK),
            )

        def weave(copy, woven, planes):
            copy(woven.rearrange("p (c i) t -> p c t i", i=PACK), planes.rearrange("p t (c i) -> p c t i", i=PACK))

        def quantise_weights(codes, scales, dealt, t0, t1):
            nc.vector.quantize_mx(out=codes.bitcast(FP8X4), scales=scales, in_=dealt[:, t0 * PACK * P : t1 * PACK * P])

        def quantise_woven(codes, scales, woven):
            nc.vector.quantize_mx(out=codes.bitcast(FP8X4), scales=scales, in_=woven[:].rearrange("p c t -> p (c t)"))

        def product(dst, weights, codes, scales):
            nc.tensor.matmul_mx(
                out=dst,
                lhsT=weights[0].bitcast(FP8X4),
                lhsT_scale=weights[1],
                rhs=codes.bitcast(FP8X4),
                rhs_scale=scales,
                start=True,
                stop=True,
            )

        offs_t = sbuf("offs_t", [P, S // GROUP], U16)
        n1_t = sbuf("n1_t", [P, W // GROUP], U16)
        n2_t = sbuf("n2_t", [P, W // GROUP], U16)
        n3_t = sbuf("n3_t", [P, S // GROUP], U16)
        n4_t = sbuf("n4_t", [P, S // GROUP], U16)
        w1_raw = sbuf("w1_raw", [P, PACK, H], F32)
        w2_raw = [sbuf("w2_raw%d" % r, [P, 2, H], F32) for r in range(2)]
        x_all = sbuf("x_all", [P, T], I32)
        xs_all = sbuf("xs_all", [P, T], U8)
        gain = sbuf("gain", [P, PACK], F32)

        xs_rows = sbuf("xs_rows", [P, T // 4], I32)
        live = [slice(QUADRANT * q, QUADRANT * q + 4) for q in range(P // QUADRANT)]
        for q, rows in enumerate(live):
            nc.sync.dma_start(xs_rows[rows, :], x_scales[0, 4 * q : 4 * q + 4, :].bitcast(I32))
        nc.sync.dma_start(offs_t[:], offs)
        nc.sync.dma_start(w1_raw[:], w1.rearrange("(p j) c -> p j c", j=PACK))
        nc.sync.dma_start(x_all[:], x_words[0].rearrange("p n t -> p (n t)").bitcast(I32))
        nc.sync.dma_start(gain[:], gn.rearrange("(p t) o -> p (t o)", t=PACK))
        w2_rows = w2.rearrange("(p j) c -> p j c", j=PACK)
        nc.sync.dma_start(w2_raw[0][:], w2_rows[:, 0:2, :])
        nc.sync.dma_start(n1_t[:], n1)
        nc.sync.dma_start(n2_t[:], n2)
        nc.sync.dma_start(w2_raw[1][:], w2_rows[:, 2:4, :])
        nc.sync.dma_start(n3_t[:], n3)
        nc.sync.dma_start(n4_t[:], n4)
        nc.vector.memset(xs_all[:].bitcast(I32), 0)
        for rows in live:
            nc.vector.tensor_copy(xs_all[rows, :].bitcast(I32), xs_rows[rows, :])

        xs = sbuf("xs", [P, S], U8)
        nc.vector.tensor_copy(xs[:], xs_all[:].indirect(offs_t[:]))
        w1_dealt = sbuf("w1_dealt", [P, PACK * H], BF16)
        deal(nc.vector.tensor_copy, w1_dealt, w1_raw)
        w1_q = sbuf("w1_q", [P, H], U32)
        w1_s = sbuf("w1_s", [P, H], U8)
        quantise_weights(w1_q[:, 0:P], w1_s[:, 0:P], w1_dealt, 0, 1)
        w1_tiles = [(w1_q[:, t * P : (t + 1) * P], w1_s[:, t * P : (t + 1) * P]) for t in range(PACK)]
        ident = sbuf("ident", [P, P], F32)
        make_identity(nc, ident[:])

        twice_step = sbuf("twice_step", [P, PACK], F32)
        sign = sbuf("sign", [P, PACK], F32)
        size = sbuf("size", [P, PACK], F32)
        neg_size = sbuf("neg_size", [P, PACK], F32)
        soft_step = sbuf("soft_step", [P, PACK], F32)
        nc.scalar.activation(soft_step[:], gain[:], ACT.Sigmoid, scale=STEEP)
        nc.gpsimd.tensor_scalar(twice_step[:], soft_step[:], 0.5, 2.0, ALU.is_ge, ALU.mult)
        nc.gpsimd.tensor_scalar(sign[:], twice_step[:], 1.0, -1.0, ALU.mult, ALU.add)
        nc.gpsimd.tensor_tensor(size[:], gain[:], sign[:], ALU.mult)
        nc.gpsimd.tensor_scalar(neg_size[:], size[:], -1.0, 0.0, ALU.mult, ALU.add)

        halves = [slice(u * HALF, (u + 1) * HALF) for u in range(2)]
        half_lists = [slice(u * HALF // GROUP, (u + 1) * HALF // GROUP) for u in range(2)]
        pieces = [(0, halves[0]), (0, halves[1])] + [(t, slice(0, S)) for t in range(1, PACK)]
        xq = sbuf("xq", [P, S], U32)
        for u in range(2):
            nc.vector.tensor_copy(xq[:, halves[u]], x_all[:].bitcast(U32).indirect(offs_t[:, half_lists[u]]))
        quantise_weights(w1_q[:, P : 2 * P], w1_s[:, P : 2 * P], w1_dealt, 1, 2)
        quantise_weights(w1_q[:, 2 * P :], w1_s[:, 2 * P :], w1_dealt, 2, PACK)
        y_ps = [bank(i, [P, cols.stop - cols.start]) for i, (t, cols) in enumerate(pieces)]
        for (t, cols), ps in zip(pieces, y_ps):
            product(ps[:], w1_tiles[t], xq[:, cols], xs[:, cols])

        ds = [sbuf("ds%d" % t, [P, S], F32) for t in range(PACK)]
        slots = sbuf("slots", [P, PACK + 1, S], BF16)
        w2_signed = slots[:, 1 : PACK + 1, :]
        z_planes = slots[:, 0:PACK, :]
        w2_dealt = sbuf("w2_dealt", [P, PACK * H], BF16)
        for j in range(2):
            nc.vector.tensor_scalar(w2_signed[:, j, :], w2_raw[0][:, j, :], sign[:, j : j + 1], None, ALU.mult)
        y_keep = sbuf("y_keep", [P, PACK, S], F32)
        gate = [sbuf("gate%d" % t, [P, W], F32) for t in range(PACK)]
        pa = [sbuf("pa%d" % t, [P, W], F32) for t in range(PACK)]

        def fetch(t):
            for (plane, cols), ps in zip(pieces, y_ps):
                if plane == t:
                    nc.scalar.copy(ds[t][:, cols], ps[:])
            if t > 0:
                nc.sync.dma_start(y_keep[:, t, :], ds[t][:])
            nc.vector.tensor_copy(pa[t][:], ds[t][:].indirect(n1_t[:]))

        def fold(t):
            nc.scalar.activation(gate[t][:], ds[t][:].indirect(n2_t[:]), ACT.Sigmoid)
            nc.vector.tensor_tensor(ds[t][:].indirect(n2_t[:]), pa[t][:], gate[t][:], ALU.mult)

        fetch(0)
        fold(0)
        fetch(1)
        for t in range(1, PACK):
            if t + 1 < PACK:
                fetch(t + 1)
            fold(t)
        for j in range(2, PACK):
            nc.scalar.activation(w2_signed[:, j, :], w2_raw[1][:, j - 2, :], ACT.Copy, scale=sign[:, j : j + 1])

        last = PACK - 1
        for t in range(last):
            nc.scalar.activation(z_planes[:, t, :], ds[t][:], ACT.Copy, scale=size[:, t : t + 1])
            if t == 0:
                deal(nc.scalar.copy, w2_dealt, w2_signed)
        last_size = size[:, last:PACK]
        nc.scalar.activation(z_planes[:, last, halves[1]], ds[last][:, halves[1]], ACT.Copy, scale=last_size)
        w2_q0 = sbuf("w2_q0", [P, P], U32)
        w2_s0 = sbuf("w2_s0", [P, P], U8)
        quantise_weights(w2_q0[:], w2_s0[:], w2_dealt, 0, 1)
        nc.vector.tensor_scalar(z_planes[:, last, halves[0]], ds[last][:, halves[0]], last_size, None, ALU.mult)

        z_woven = [sbuf("z_woven%d" % u, [P, HALF, PACK], BF16) for u in range(2)]
        z_q = sbuf("z_q", [P, S], U32)
        z_s = sbuf("z_s", [P, S], U8)
        weave(nc.vector.tensor_copy, z_woven[0][:], z_planes[:, :, halves[0]])
        weave(nc.scalar.copy, z_woven[1][:, 0:QUARTER, :], z_planes[:, :, HALF : HALF + QUARTER])
        weave(nc.vector.tensor_copy, z_woven[1][:, QUARTER:HALF, :], z_planes[:, :, HALF + QUARTER : S])
        for u in range(2):
            quantise_woven(z_q[:, halves[u]], z_s[:, halves[u]], z_woven[u])
        w2_q = sbuf("w2_q", [P, H - P], U32, tag="z_woven1")
        w2_s = sbuf("w2_s", [P, H - P], U8)
        quantise_weights(w2_q[:, 0:P], w2_s[:, 0:P], w2_dealt, 1, 2)
        quantise_weights(w2_q[:, P:], w2_s[:, P:], w2_dealt, 2, PACK)
        w2_tiles = [(w2_q0[:], w2_s0[:])]
        w2_tiles.extend((w2_q[:, t * P : (t + 1) * P], w2_s[:, t * P : (t + 1) * P]) for t in range(PACK - 1))

        h_banks = (5, 6, 7, 2, 3)
        window = [sbuf("window%d" % t, [P, S], F32) for t in range(PACK)]
        plain = [[sbuf("plain%d_%d" % (t, u), [P, HALF], F32) for u in range(2)] for t in range(PACK)]
        for (t, cols), index in zip(pieces, h_banks):
            ps = bank(index, [P, cols.stop - cols.start])
            product(ps[:], w2_tiles[t], z_q[:, cols], z_s[:, cols])
            scale = neg_size[:, t : t + 1]
            nc.scalar.activation(window[t][:, cols], ps[:], ACT.Copy, scale=scale)
            if cols.start == 0 and t == 0:
                nc.vector.tensor_copy(plain[t][0][:], window[t][:, halves[0]])
            elif cols.start == 0:
                nc.scalar.activation(plain[t][0][:], ps[:, halves[0]], ACT.Copy, scale=scale)
            if cols.stop == S:
                nc.sync.dma_start(plain[t][1][:], window[t][:, halves[1]])
        y_plane0 = sbuf("y_plane0", [P, S], F32, tag="slots")
        for u in range(2):
            nc.scalar.copy(y_plane0[:, halves[u]], y_ps[u][:])
        nc.sync.dma_start(y_keep[:, 0, :], y_plane0[:])

        out_planes = out.rearrange("(p t) s -> p t s", t=PACK)
        pairs = [slice(2 * r, 2 * r + 2) for r in range(2)]

        def differences(dst, list_t, t, u):
            nc.vector.tensor_tensor(dst, window[t][:].indirect(list_t[:, half_lists[u]]), plain[t][u][:], ALU.subtract)

        def last_product(name, woven, n, banks):
            codes = sbuf(name + "_q", [P, n], U32)
            scales = sbuf(name + "_s", [P, n], U8)
            quantise_woven(codes[:], scales[:], woven)
            sums = [bank(i, [P, 2, n]) for i in banks]
            for t in range(PACK):
                product(sums[t // 2][:, t % 2, :], w2_tiles[t], codes[:], scales[:])
            return sums

        def finish(name, sums, a, b, tag=None):
            res = sbuf(name, [P, PACK, b - a], F32, tag=tag)
            for pair, ps in zip(pairs, sums):
                nc.vector.scalar_tensor_tensor(res[:, pair, :], y_keep[:, pair, a:b], 1.5, ps[:], ALU.mult, ALU.add)
                nc.sync.dma_start(out_planes[:, pair, a:b], res[:, pair, :])

        d4_first = sbuf("d4_first", [P, PACK, HALF], F32)
        d3_first = sbuf("d3_first", [P, PACK, HALF], F32)
        r4_first = sbuf("r4_first", [P, PACK, HALF], F32)
        r3_first = sbuf("r3_first", [P, PACK, HALF], F32)
        for t in range(PACK):
            differences(d4_first[:, t, :], n4_t, t, 0)
            differences(d3_first[:, t, :], n3_t, t, 0)
        for some in (pairs[0], slice(2, last), slice(last, PACK)):
            nc.scalar.activation(r4_first[:, some, :], d4_first[:, some, :], ACT.Relu, scale=-0.5)
            nc.scalar.activation(r3_first[:, some, :], d3_first[:, some, :], ACT.Relu)

        blocks = HALF // P
        first_woven = sbuf("first_woven", [P, HALF, PACK], BF16)
        by_column = [bank(i, [P, PACK, P]) for i in (4, 5)]
        for t in range(PACK):
            for b in range(blocks):
                cols = slice(b * P, (b + 1) * P)
                dst = by_column[b][:, t, :]
                nc.tensor.matmul(dst, r4_first[:, t, cols], ident[:], start=True, stop=False, is_transpose=True)
                nc.tensor.matmul(dst, r3_first[:, t, cols], ident[:], start=False, stop=True, is_transpose=True)
        words = bank(7, [P, blocks, 2, P])
        rounded = sbuf("rounded", [P, blocks, 2, P, 2], BF16)
        for b in range(blocks):
            nc.scalar.copy(rounded[:, b], by_column[b][:].rearrange("p (e r) m -> p e m r", r=2))
            as_words = rounded[:, b].rearrange("p e m r -> p (e m r)").bitcast(F32)
            for e in range(2):
                nc.tensor.transpose(words[:, b, e, :], as_words[:, e * P : (e + 1) * P], ident[:])
        nc.scalar.copy(
            first_woven[:].rearrange("p c t -> p (c t)").bitcast(F32).rearrange("p (b c e) -> p b c e", b=blocks, e=2),
            words[:].rearrange("p b e c -> p b c e"),
        )
        sums_first = last_product("first", first_woven, HALF, (3, 4))

        d4_second = sbuf("d4_second", [P, PACK, HALF], F32, tag="plain3_0")
        d3_second = sbuf("d3_second", [P, PACK, HALF], F32, tag="d4_first")
        r4_second = [sbuf("r4_second0", [P, 2, HALF], F32), sbuf("r4_second1", [P, 2, HALF], F32, tag="rounded")]
        z2_planes = sbuf("z2_planes", [P, PACK, HALF], BF16)
        for t in range(PACK):
            differences(d4_second[:, t, :], n4_t, t, 1)
        for pair, r4 in zip(pairs, r4_second):
            nc.scalar.activation(r4[:], d4_second[:, pair, :], ACT.Relu, scale=-0.5)
        for t in range(PACK):
            differences(d3_second[:, t, :], n3_t, t, 1)
        for pair, r4 in zip(pairs, r4_second):
            nc.vector.scalar_tensor_tensor(z2_planes[:, pair, :], d3_second[:, pair, :], 0.0, r4[:], ALU.max, ALU.add)
        third_woven = sbuf("third_woven", [P, QUARTER, PACK], BF16)
        fourth_woven = sbuf("fourth_woven", [P, QUARTER, PACK], BF16)
        weave(nc.scalar.copy, third_woven[:], z2_planes[:, :, 0:QUARTER])
        weave(nc.vector.tensor_copy, fourth_woven[:], z2_planes[:, :, QUARTER:HALF])
        sums_fourth = last_product("fourth", fourth_woven, QUARTER, (5, 7))
        sums_third = last_product("third", third_woven, QUARTER, (0, 1))
        finish("res_first", sums_first, 0, HALF, tag="plain3_0")
        finish("res_fourth", sums_fourth, HALF + QUARTER, S)
        finish("res_third", sums_third, HALF, HALF + QUARTER)
